import numpy as np
import ml_dtypes


def mxq(x, axis, fmt="e4m3"):
    dtype, down = {"e4m3": (ml_dtypes.float8_e4m3fn, 7), "e5m2": (ml_dtypes.float8_e5m2, 14)}[fmt]
    v = np.moveaxis(np.asarray(x, np.float32).astype(ml_dtypes.bfloat16).astype(np.float64), axis, -1)
    blocks = v.reshape(v.shape[:-1] + (-1, 32))
    amax = np.abs(blocks).max(-1, keepdims=True)
    byte = np.maximum(np.where(amax > 0, np.frexp(amax)[1] - 1 + 127, 0) - down, 1)
    scale = np.exp2(byte - 127.0)
    codes = (blocks / scale).astype(np.float32).astype(dtype).astype(np.float64)
    return np.moveaxis((codes * scale).reshape(v.shape), -1, axis)


WIDE = False


def mx_kscale(k):
    if not WIDE:
        return np.ones(k)
    levels = np.array([10, -10, 5, -5, 0])
    if k % 512:
        return np.exp2(np.random.permutation(np.resize(levels, k // 32))).repeat(32)
    a = np.empty((k // 512, 16))
    for p in range(k // 512):
        a[p, :8] = np.random.permutation(np.resize(levels, 8))
        for g in range(8):
            far = levels[np.abs(levels - a[p, g]) >= 10]
            a[p, g + 8] = far[np.random.randint(len(far))]
    return np.exp2(a.ravel()).repeat(32)


def f64(x):
    return np.asarray(x).astype(np.float64)


def striped(idx):
    return np.tile(np.asarray(idx).reshape(-1, 16).T, (8, 1)).astype(np.uint16)


def unstriped(offs):
    return offs[:16].T.reshape(-1).astype(np.int64)


E2M1 = np.array([0.0, 0.5, 1.0, 1.5, 2.0, 3.0, 4.0, 6.0, -0.0, -0.5, -1.0, -1.5, -2.0, -3.0, -4.0, -6.0])


def pack_weight(w, fmt):
    k, n = w.shape
    w = f64(np.asarray(w, np.float32).astype(ml_dtypes.bfloat16)).reshape(k // 32, 32, n)
    amax = np.abs(w).max(1)
    if fmt == "e4m3":
        byte = np.frexp(amax)[1] - 1 + 127 - 7
    else:
        mant, ex = np.frexp(amax / 6.0)
        byte = np.where(mant > 0.5, ex, ex - 1) + 127
    byte = np.clip(np.where(amax > 0, byte, 1), 1, 254)
    scaled = (w * np.exp2(127.0 - byte)[:, None, :]).reshape(k, n).astype(np.float32)
    by_word = np.ascontiguousarray(scaled.reshape(k // 512, 128, 4, n).transpose(0, 1, 3, 2))
    if fmt == "e4m3":
        words = by_word.astype(ml_dtypes.float8_e4m3fn).view(np.uint8)
    else:
        c = by_word.astype(ml_dtypes.float4_e2m1fn).view(np.uint8) & 0xF
        words = (c[..., 0::2] | (c[..., 1::2] << 4)).reshape(k // 512, 128, 2 * n)
    return np.ascontiguousarray(words), np.ascontiguousarray(byte.astype(np.uint8).reshape(k // 512, 16, n))


def unpack_weight(words, scales, fmt):
    g, _, n = scales.shape
    words = np.ascontiguousarray(words).reshape(g, 128, n, -1)
    if fmt == "e4m3":
        vals = words.view(ml_dtypes.float8_e4m3fn).astype(np.float64)
    else:
        nib = np.empty((g, 128, n, 4), np.uint8)
        nib[..., 0::2] = words & 0xF
        nib[..., 1::2] = words >> 4
        vals = E2M1[nib]
    vals = vals * np.repeat(np.exp2(scales.astype(np.float64) - 127.0), 8, axis=1)[..., None]
    return vals.transpose(0, 1, 3, 2).reshape(g * 512, n)


B, N, T, D, DV, NQ = 2, 512, 2048, 1024, 256, 256


def setup_inputs():
    n = np.random.standard_normal
    seg = T // B
    idx = np.concatenate([b * seg + np.random.permutation(seg)[:N] for b in range(B)])
    s = mx_kscale(D)[:, None]
    u = np.ones(T)
    u[idx] = mx_kscale(B * N)
    r = np.random.uniform(0.5, 2.0, T)
    qp = [pack_weight(x, "e4m3") for x in n((B, D, NQ)) * s * (0.80 / np.sqrt(D))]
    k = n((D, T)) / s
    v = n((DV, T)) / (u * r)
    kp = pack_weight(k, "e2m1")
    return {
        "q_words": np.stack([x[0] for x in qp]),
        "q_scales": np.stack([x[1] for x in qp]),
        "k_words": np.ascontiguousarray(kp[0].reshape(D // 1024, 2, 128, T, 2).transpose(0, 2, 3, 1, 4)).reshape(D // 1024, 128, T, 4),
        "k_scales": kp[1],
        "vT": v.astype(np.float32),
        "vs": np.tile(u * r, (128, 1)).astype(np.float32),
        "sink": (2.0 + 3.0 * n((B, NQ, 1))).astype(np.float32),
        "og": n((B, NQ, DV)).astype(np.float32),
        "offs": striped(idx),
    }


def reference(q_words, q_scales, k_words, k_scales, vT, vs, sink, og, offs):
    idx = unstriped(offs)
    k = unpack_weight(k_words.reshape(D // 1024, 128, T, 2, 2).transpose(0, 3, 1, 2, 4).reshape(D // 512, 128, 2 * T), k_scales, "e2m1")
    v = f64(vT)
    pick = lambda x: x[:, idx].reshape(x.shape[0], B, N).transpose(1, 0, 2)
    q = np.stack([unpack_weight(q_words[b], q_scales[b], "e4m3") for b in range(B)])
    score = q.transpose(0, 2, 1) @ pick(k)
    m = np.maximum(score.max(-1, keepdims=True), f64(sink))
    p = np.exp(score - m)
    total = p.sum(-1, keepdims=True) + np.exp(f64(sink) - m)
    w = p * pick(f64(vs))[:, :1, :]
    y = mxq(w, 2, "e4m3") @ mxq(pick(v).transpose(0, 2, 1), 1, "e4m3")
    y = y / total
    y = y / (1.0 + np.exp(-f64(og)))
    return y

@@ -1,0 +1,254 @@
+from contextlib import ExitStack
+
+import concourse.mybir as mybir
+from concourse.masks import make_identity
+
+B, N, T, D, DV, NQ = 2, 512, 2048, 1024, 256, 256
+FLOPS = 2 * B * NQ * N * (D + DV)
+
+F32 = mybir.dt.float32
+BF16 = mybir.dt.bfloat16
+I32 = mybir.dt.int32
+U32 = mybir.dt.uint32
+U16 = mybir.dt.uint16
+U8 = mybir.dt.uint8
+FP8X4 = mybir.dt.float8_e4m3fn_x4
+FP4X4 = mybir.dt.float4_e2m1fn_x4
+ALU = mybir.AluOpType
+ACT = mybir.ActivationFunctionType
+
+P = 128
+PACK = 4
+PASSES = D // (P * PACK)
+SEG = T // B
+HALVES = NQ // P
+TILES = B * HALVES
+LIST_COLS = N // 16
+ROW = N + 8
+
+
+def tile_attend_soft_sink_gate_segb2q256n512t2048_kernel(
+    tc, q_words, q_scales, k_words, k_scales, vT, vs, sink, og, offs, out
+):
+    nc = tc.nc
+    with ExitStack() as ctx:
+        keep = ctx.enter_context(tc.tile_pool(name="keep", bufs=1))
+        psum = ctx.enter_context(tc.psum_pool(name="psum", bufs=1))
+
+        def sb(name, shape, dtype):
+            return keep.tile(shape, dtype, name=name, align_bytes=64)
+
+        offsets = keep.tile([P, B * LIST_COLS], U16, name="offsets")
+        k_pool = sb("k_pool", [P, T], I32)
+        ks_pool = sb("ks_pool", [P, T], U8)
+        vs_pool = sb("vs_pool", [P, T], F32)
+        v_pairs = sb("v_pairs", [P, 2 * T], BF16)
+        v_raw = [sb(f"v_raw{b}", [P, 2, SEG], F32) for b in range(B)]
+        q_codes = sb("q_codes", [P, B * PASSES, NQ], I32)
+        q_planes = sb("q_planes", [P, B * PASSES * NQ], U8)
+        ks_got = sb("ks_got", [P, B * N], U8)
+        ks_moved = sb("ks_moved", [P, B * N], U8)
+        sink_cols = sb("sink_cols", [P, TILES], F32)
+        og_sb = sb("og_sb", [P, TILES, DV], F32)
+        half_tanh = sb("half_tanh", [P, TILES * DV], F32)
+        gate = sb("gate", [P, TILES * DV], F32)
+        neg_logits = sb("neg_logits", [P, TILES, ROW], F32)
+        ident = sb("ident", [P, P], F32)
+
+        totals = sb("totals", [P, TILES], F32)
+        inverses = sb("inverses", [P, TILES], F32)
+        warm = sb("warm", [P, 2], F32)
+
+        nc.gpsimd.memset(ks_pool[:].bitcast(I32), 0)
+        nc.vector.memset(warm[:, 0:1], 0.0)
+        nc.vector.memset(q_planes[:].bitcast(I32), 0)
+        nc.vector.memset(ks_moved[:].bitcast(I32), 0)
+        nc.vector.memset(vs_pool[:], 0.0)
+        make_identity(nc, ident[:])
+
+        k_flat = k_words[0].rearrange("p t r -> p (t r)").bitcast(I32)
+        v_rows = vT.rearrange("(p h) t -> p h t", h=2)
+
+        nc.sync.dma_start(offsets[:], offs)
+        for quad in range(4):
+            nc.scalar.dma_start(
+                out=ks_pool[32 * quad : 32 * quad + 8, :].bitcast(I32),
+                in_=k_scales[:, 4 * quad : 4 * quad + 4, :].bitcast(I32),
+            )
+        nc.scalar.activation(out=warm[:, 1:2], in_=warm[:, 0:1], func=ACT.Exp)
+        nc.sync.dma_start(out=k_pool[:, 0:SEG], in_=k_flat[:, 0:SEG])
+        nc.sync.dma_start(out=v_raw[0][:], in_=v_rows[:, :, 0:SEG])
+        nc.sync.dma_start(out=k_pool[:, SEG:T], in_=k_flat[:, SEG:T])
+        nc.sync.dma_start(out=q_codes[:], in_=q_words.rearrange("b o p q r -> p (b o) (q r)").bitcast(I32))
+        for quad in range(4):
+            nc.sync.dma_start(
+                out=q_planes[32 * quad : 32 * quad + 4, :].bitcast(I32).rearrange("f (g q) -> f g q", g=B * PASSES),
+                in_=q_scales[:, :, 4 * quad : 4 * quad + 4, :].rearrange("b o f q -> f (b o) q").bitcast(I32),
+            )
+        nc.sync.dma_start(out=vs_pool[0:1, :], in_=vs[0:1, :])
+        with nc.allow_non_contiguous_dma(reason="one sink logit to a partition"):
+            nc.sync.dma_start(out=sink_cols[:], in_=sink.rearrange("b (h p) one -> p (b h one)", p=P))
+        nc.sync.dma_start(out=v_raw[1][:], in_=v_rows[:, :, SEG:T])
+        nc.sync.dma_start(out=og_sb[:], in_=og.rearrange("b (h p) e -> p (b h) e", p=P))
+
+        def listed(b):
+            return offsets[:, b * LIST_COLS : (b + 1) * LIST_COLS]
+
+        nc.vector.tensor_copy(ks_got[:], ks_pool[:].indirect(offsets[:]))
+        for quad in range(4):
+            nc.scalar.dma_start(
+                out=ks_moved[32 * quad : 32 * quad + 4, :].bitcast(I32),
+                in_=ks_got[32 * quad + 4 : 32 * quad + 8, :].bitcast(I32),
+            )
+        k_planes = [ks_got, ks_moved]
+
+        def keys(b):
+            k_got = sb(f"k_got{b}", [P, N], U32)
+            nc.vector.tensor_copy(k_got[:], k_pool[:, 0 : (b + 1) * SEG].bitcast(U32).indirect(listed(b)))
+            k_codes = sb(f"k_codes{b}", [P, PASSES, 2 * N], U8)
+            nc.vector.tensor_copy(
+                out=k_codes[:].bitcast(U16).rearrange("p o (c i) -> p c o i", i=8),
+                in_=k_got[:].bitcast(U16).rearrange("p (c i o) -> p c o i", i=8, o=PASSES),
+            )
+            return k_codes
+
+        def scores(b, h, k_codes):
+            acc = psum.tile([P, N], F32, name="score", tag="acc", bufs=4)
+            for o in range(PASSES):
+                first = (b * PASSES + o) * NQ + h * P
+                nc.tensor.matmul_mx(
+                    out=acc[:],
+                    lhsT=q_codes[:, b * PASSES + o, h * P : (h + 1) * P].bitcast(FP8X4),
+                    lhsT_scale=q_planes[:, first : first + P],
+                    rhs=k_codes[:, o, :].bitcast(FP4X4),
+                    rhs_scale=k_planes[o][:, b * N : (b + 1) * N],
+                    start=(o == 0),
+                    stop=(o == PASSES - 1),
+                )
+            return acc
+
+        def softmax(j, acc):
+            neg_max = sb(f"neg_max{j}", [P, 1], F32)
+            nc.vector.tensor_scalar(
+                out=neg_logits[:, j, 0:N].rearrange("p (t s) -> p t s", t=PACK),
+                in0=acc[:].rearrange("p (s t) -> p t s", t=PACK),
+                scalar1=-1.0,
+                scalar2=neg_logits[:, j, N : N + 1],
+                op0=ALU.mult,
+                op1=ALU.min,
+                accum_out=neg_max[:],
+            )
+            probs = sb(f"probs{j}", [P, ROW], F32)
+            nc.scalar.activation(
+                out=probs[:, 0 : N + 1],
+                in_=neg_logits[:, j, 0 : N + 1],
+                func=ACT.Exp,
+                bias=neg_max[:],
+                scale=-1.0,
+                accum_out=totals[:, j : j + 1],
+            )
+            turned = psum.tile([P, PACK, P], F32, name="probs_turned", tag="probs_turned", bufs=2)
+            for t in range(PACK):
+                nc.tensor.transpose(turned[:, t, :], probs[:, t * P : (t + 1) * P], ident[:])
+            return turned
+
+        def cast_values(b):
+            nc.scalar.activation(
+                out=v_pairs[:, 2 * b * SEG : 2 * (b + 1) * SEG].rearrange("p (t h) -> p t h", h=2),
+                in_=v_raw[b][:].rearrange("p h t -> p t h"),
+                func=ACT.Copy,
+            )
+
+        def token_scales(b):
+            vs_got = sb(f"vs_got{b}", [P, N], F32)
+            nc.vector.tensor_copy(vs_got[:], vs_pool[:].indirect(listed(b)))
+            turned = psum.tile([P, PACK, P], F32, name="vs_turned", tag="turned", bufs=2)
+            for t in range(PACK):
+                nc.tensor.transpose(turned[:, t, :], vs_got[:, t:N:PACK], ident[:])
+            vs_cols = sb(f"vs_cols{b}", [P, PACK], F32)
+            nc.scalar.copy(out=vs_cols[:], in_=turned[:, :, 0])
+            return vs_cols
+
+        def gather_values(b):
+            v_got = sb(f"v_got{b}", [P, N], U32)
+            nc.vector.tensor_copy(v_got[:], v_pairs[:, 0 : 2 * (b + 1) * SEG].bitcast(U32).indirect(listed(b)))
+            turned = psum.tile([P, PACK, P], F32, name="v_turned", tag="turned", bufs=2)
+            for t in range(PACK):
+                nc.tensor.transpose(turned[:, t, :], v_got[:].bitcast(F32)[:, t:N:PACK], ident[:])
+            v_woven = sb(f"v_woven{b}", [P, DV, PACK], BF16)
+            nc.scalar.copy(out=v_woven[:], in_=turned[:].bitcast(BF16).rearrange("p t e -> p e t"))
+            return v_woven
+
+        def quantize(name, woven, cols):
+            codes = sb(f"{name}_codes", [P, cols], U32)
+            plane = sb(f"{name}_plane", [P, cols], U8)
+            nc.vector.quantize_mx(
+                out=codes[:].bitcast(FP8X4), scales=plane[:], in_=woven[:].rearrange("p c t -> p (c t)")
+            )
+            return codes, plane
+
+        def weigh(j, turned, vs_cols):
+            w_woven = sb(f"w_woven{j}", [P, P, PACK], BF16)
+            nc.vector.tensor_tensor(
+                out=w_woven[:],
+                in0=turned[:].rearrange("p t q -> p q t"),
+                in1=vs_cols[:].unsqueeze(1).to_broadcast([P, P, PACK]),
+                op=ALU.mult,
+            )
+            return w_woven
+
+        def mix(w_mx, v_mx):
+            acc = psum.tile([P, DV], F32, name="mixed", tag="acc", bufs=4)
+            nc.tensor.matmul_mx(
+                out=acc[:],
+                lhsT=w_mx[0][:].bitcast(FP8X4),
+                lhsT_scale=w_mx[1][:],
+                rhs=v_mx[0][:].bitcast(FP8X4),
+                rhs_scale=v_mx[1][:],
+                start=True,
+                stop=True,
+            )
+            return acc
+
+        def finish(j, acc):
+            result = sb(f"result{j}", [P, DV], F32)
+            nc.vector.scalar_tensor_tensor(
+                out=result[:],
+                in0=acc[:],
+                scalar=inverses[:, j : j + 1],
+                in1=gate[:, j * DV : (j + 1) * DV],
+                op0=ALU.mult,
+                op1=ALU.mult,
+            )
+            b, h = divmod(j, HALVES)
+            nc.sync.dma_start(out=out[b, h * P : (h + 1) * P, :], in_=result[:])
+
+        nc.scalar.activation(out=neg_logits[:, :, N], in_=sink_cols[:], func=ACT.Copy, scale=-1.0)
+        k_codes = [keys(b) for b in range(B)]
+        accs = [scores(b, h, k_codes[b]) for b in range(B) for h in range(HALVES)]
+        cast_values(0)
+        soft = [softmax(j, accs[j]) for j in range(HALVES)]
+        vs_cols = [token_scales(0)]
+        cast_values(1)
+        v_woven = [gather_values(0)]
+        soft.append(softmax(2, accs[2]))
+        w_woven = [weigh(0, soft[0], vs_cols[0])]
+        soft.append(softmax(3, accs[3]))
+        w_woven.append(weigh(1, soft[1], vs_cols[0]))
+        vs_cols.append(token_scales(1))
+        v_mx = [quantize("v0", v_woven[0], DV)]
+        w_mx = [quantize(f"w{j}", w_woven[j], P) for j in range(HALVES)]
+        v_woven.append(gather_values(1))
+        mixed = [mix(w_mx[j], v_mx[0]) for j in range(HALVES)]
+        nc.scalar.activation(out=half_tanh[:], in_=og_sb[:].rearrange("p j e -> p (j e)"), func=ACT.Tanh, scale=0.5)
+        nc.gpsimd.tensor_scalar(out=gate[:], in0=half_tanh[:], scalar1=0.5, scalar2=0.5, op0=ALU.mult, op1=ALU.add)
+        w_woven.append(weigh(2, soft[2], vs_cols[1]))
+        w_woven.append(weigh(3, soft[3], vs_cols[1]))
+        nc.vector.reciprocal(inverses[:], totals[:])
+        finish(0, mixed[0])
+        v_mx.append(quantize("v1", v_woven[1], DV))
+        for j in range(HALVES, TILES):
+            w_mx.append(quantize(f"w{j}", w_woven[j], P))
+            mixed.append(mix(w_mx[j], v_mx[1]))
+        for j in range(1, TILES):
+            finish(j, mixed[j])

@@ -35,80 +35,84 @@ def tile_attend_soft_sink_gate_segb2q256n512t2048_kernel(
         keep = ctx.enter_context(tc.tile_pool(name="keep", bufs=1))
         psum = ctx.enter_context(tc.psum_pool(name="psum", bufs=1))
 
-        def sb(name, shape, dtype):
-            return keep.tile(shape, dtype, name=name, align_bytes=64)
+        def sb(name, shape, dtype, tag=""):
+            return keep.tile(shape, dtype, name=name, tag=tag or name, align_bytes=64)
 
         offsets = keep.tile([P, B * LIST_COLS], U16, name="offsets")
         k_pool = sb("k_pool", [P, T], I32)
-        ks_pool = sb("ks_pool", [P, T], U8)
+        ks_pool = sb("ks_pool", [P, T], U8, tag="ks_then_v")
         vs_pool = sb("vs_pool", [P, T], F32)
         v_pairs = sb("v_pairs", [P, 2 * T], BF16)
-        v_raw = [sb(f"v_raw{b}", [P, 2, SEG], F32) for b in range(B)]
-        q_codes = sb("q_codes", [P, B * PASSES, NQ], I32)
+        neg_logits = sb("neg_logits", [P, TILES, ROW], F32)
         q_planes = sb("q_planes", [P, B * PASSES * NQ], U8)
         ks_got = sb("ks_got", [P, B * N], U8)
-        ks_moved = sb("ks_moved", [P, B * N], U8)
-        sink_cols = sb("sink_cols", [P, TILES], F32)
+        k_planes = sb("k_planes", [P, PASSES * B * N], U8)
+        sink_rows = sb("sink_rows", [P, P], F32)
         og_sb = sb("og_sb", [P, TILES, DV], F32)
-        half_tanh = sb("half_tanh", [P, TILES * DV], F32)
+        half_tanh = sb("half_tanh", [P, TILES * DV], F32, tag="tanh_then_q")
         gate = sb("gate", [P, TILES * DV], F32)
-        neg_logits = sb("neg_logits", [P, TILES, ROW], F32)
         ident = sb("ident", [P, P], F32)
-
         totals = sb("totals", [P, TILES], F32)
         inverses = sb("inverses", [P, TILES], F32)
         warm = sb("warm", [P, 2], F32)
 
-        nc.gpsimd.memset(ks_pool[:].bitcast(I32), 0)
         nc.vector.memset(warm[:, 0:1], 0.0)
-        nc.vector.memset(q_planes[:].bitcast(I32), 0)
-        nc.vector.memset(ks_moved[:].bitcast(I32), 0)
-        nc.vector.memset(vs_pool[:], 0.0)
+        nc.vector.memset(ks_pool[32:64, :].bitcast(I32), 0)
+        nc.vector.memset(ks_pool[64:128, :].bitcast(I32), 0)
+        nc.vector.memset(sink_rows[:], 0.0)
+        nc.vector.memset(k_planes[:].bitcast(I32), 0)
         make_identity(nc, ident[:])
+        nc.gpsimd.memset(vs_pool[:], 0.0)
+        nc.gpsimd.memset(q_planes[:].bitcast(I32), 0)
 
         k_flat = k_words[0].rearrange("p t r -> p (t r)").bitcast(I32)
         v_rows = vT.rearrange("(p h) t -> p h t", h=2)
 
-        nc.sync.dma_start(offsets[:], offs)
-        for quad in range(4):
-            nc.scalar.dma_start(
-                out=ks_pool[32 * quad : 32 * quad + 8, :].bitcast(I32),
-                in_=k_scales[:, 4 * quad : 4 * quad + 4, :].bitcast(I32),
-            )
         nc.scalar.activation(out=warm[:, 1:2], in_=warm[:, 0:1], func=ACT.Exp)
-        nc.sync.dma_start(out=k_pool[:, 0:SEG], in_=k_flat[:, 0:SEG])
-        nc.sync.dma_start(out=v_raw[0][:], in_=v_rows[:, :, 0:SEG])
-        nc.sync.dma_start(out=k_pool[:, SEG:T], in_=k_flat[:, SEG:T])
-        nc.sync.dma_start(out=q_codes[:], in_=q_words.rearrange("b o p q r -> p (b o) (q r)").bitcast(I32))
-        for quad in range(4):
-            nc.sync.dma_start(
-                out=q_planes[32 * quad : 32 * quad + 4, :].bitcast(I32).rearrange("f (g q) -> f g q", g=B * PASSES),
-                in_=q_scales[:, :, 4 * quad : 4 * quad + 4, :].rearrange("b o f q -> f (b o) q").bitcast(I32),
-            )
-        nc.sync.dma_start(out=vs_pool[0:1, :], in_=vs[0:1, :])
-        with nc.allow_non_contiguous_dma(reason="one sink logit to a partition"):
-            nc.sync.dma_start(out=sink_cols[:], in_=sink.rearrange("b (h p) one -> p (b h one)", p=P))
-        nc.sync.dma_start(out=v_raw[1][:], in_=v_rows[:, :, SEG:T])
+        nc.sync.dma_start(offsets[:], offs)
+        nc.sync.dma_start(out=ks_pool[0:32, :].bitcast(I32), in_=k_scales.rearrange("o f t -> f o t").bitcast(I32))
         nc.sync.dma_start(out=og_sb[:], in_=og.rearrange("b (h p) e -> p (b h) e", p=P))
+        nc.sync.dma_start(out=k_pool[:, 0:SEG], in_=k_flat[:, 0:SEG])
+        nc.sync.dma_start(out=k_pool[:, SEG:T], in_=k_flat[:, SEG:T])
+        v_raw = [sb("v_raw0", [P, 2, SEG], F32)]
+        nc.sync.dma_start(out=v_raw[0][:], in_=v_rows[:, :, 0:SEG])
+        nc.scalar.dma_start(out=sink_rows[0:TILES, :], in_=sink.rearrange("b (h p) one -> (b h) (p one)", p=P))
+        nc.scalar.dma_start(out=vs_pool[0:1, :], in_=vs[0:1, :])
 
         def listed(b):
             return offsets[:, b * LIST_COLS : (b + 1) * LIST_COLS]
 
         nc.vector.tensor_copy(ks_got[:], ks_pool[:].indirect(offsets[:]))
+        v_raw.append(sb("v_raw1", [P, 2, SEG], F32, tag="ks_then_v"))
+        nc.sync.dma_start(out=v_raw[1][:], in_=v_rows[:, :, SEG:T])
         for quad in range(4):
-            nc.scalar.dma_start(
-                out=ks_moved[32 * quad : 32 * quad + 4, :].bitcast(I32),
-                in_=ks_got[32 * quad + 4 : 32 * quad + 8, :].bitcast(I32),
+            nc.sync.dma_start(
+                out=k_planes[32 * quad : 32 * quad + 4, :].bitcast(I32).rearrange("f (o n) -> f o n", o=PASSES),
+                in_=ks_got[8 * quad : 8 * quad + 8, :].bitcast(I32),
             )
-        k_planes = [ks_got, ks_moved]
+        for quad in range(4):
+            nc.sync.dma_start(
+                out=q_planes[32 * quad : 32 * quad + 4, :].bitcast(I32).rearrange("f (g q) -> f g q", g=B * PASSES),
+                in_=q_scales[:, :, 4 * quad : 4 * quad + 4, :].rearrange("b o f q -> f (b o) q").bitcast(I32),
+            )
+        nc.scalar.activation(out=half_tanh[:], in_=og_sb[:].rearrange("p j e -> p (j e)"), func=ACT.Tanh, scale=0.5)
+        nc.scalar.activation(out=gate[:], in_=half_tanh[:], func=ACT.Copy, scale=0.5, bias=0.5)
+        q_codes = sb("q_codes", [P, B * PASSES, NQ], I32, tag="tanh_then_q")
+        nc.sync.dma_start(out=q_codes[:], in_=q_words.rearrange("b o p q r -> p (b o) (q r)").bitcast(I32))
+        sink_turned = psum.tile([P, P], F32, name="sink_turned", tag="turned", bufs=4)
+        nc.tensor.transpose(sink_turned[:], sink_rows[:], ident[:])
+        nc.scalar.activation(out=neg_logits[:, :, N], in_=sink_turned[:, 0:TILES], func=ACT.Copy, scale=-1.0)
 
-        def keys(b):
-            k_got = sb(f"k_got{b}", [P, N], U32)
+        def gather_keys(b):
+            k_got = sb(f"k_got{b}", [P, N], U32, tag=f"got{b}")
             nc.vector.tensor_copy(k_got[:], k_pool[:, 0 : (b + 1) * SEG].bitcast(U32).indirect(listed(b)))
+            return k_got
+
+        def part_keys(b, k_got):
             k_codes = sb(f"k_codes{b}", [P, PASSES, 2 * N], U8)
             nc.vector.tensor_copy(
-                out=k_codes[:].bitcast(U16).rearrange("p o (c i) -> p c o i", i=8),
-                in_=k_got[:].bitcast(U16).rearrange("p (c i o) -> p c o i", i=8, o=PASSES),
+                out=k_codes[:].bitcast(U16),
+                in_=k_got[:].bitcast(U16).rearrange("p (i o) -> p o i", o=PASSES),
             )
             return k_codes
 
@@ -121,14 +125,14 @@ def tile_attend_soft_sink_gate_segb2q256n512t2048_kernel(
                     lhsT=q_codes[:, b * PASSES + o, h * P : (h + 1) * P].bitcast(FP8X4),
                     lhsT_scale=q_planes[:, first : first + P],
                     rhs=k_codes[:, o, :].bitcast(FP4X4),
-                    rhs_scale=k_planes[o][:, b * N : (b + 1) * N],
+                    rhs_scale=k_planes[:, (o * B + b) * N : (o * B + b + 1) * N],
                     start=(o == 0),
                     stop=(o == PASSES - 1),
                 )
             return acc
 
         def softmax(j, acc):
-            neg_max = sb(f"neg_max{j}", [P, 1], F32)
+            neg_max = sb(f"neg_max{j}", [P, 1], F32, tag="")
             nc.vector.tensor_scalar(
                 out=neg_logits[:, j, 0:N].rearrange("p (t s) -> p t s", t=PACK),
                 in0=acc[:].rearrange("p (s t) -> p t s", t=PACK),
@@ -147,7 +151,7 @@ def tile_attend_soft_sink_gate_segb2q256n512t2048_kernel(
                 scale=-1.0,
                 accum_out=totals[:, j : j + 1],
             )
-            turned = psum.tile([P, PACK, P], F32, name="probs_turned", tag="probs_turned", bufs=2)
+            turned = psum.tile([P, PACK, P], F32, name="probs_turned", tag="turned", bufs=4)
             for t in range(PACK):
                 nc.tensor.transpose(turned[:, t, :], probs[:, t * P : (t + 1) * P], ident[:])
             return turned
@@ -159,23 +163,24 @@ def tile_attend_soft_sink_gate_segb2q256n512t2048_kernel(
                 func=ACT.Copy,
             )
 
-        def token_scales(b):
-            vs_got = sb(f"vs_got{b}", [P, N], F32)
-            nc.vector.tensor_copy(vs_got[:], vs_pool[:].indirect(listed(b)))
-            turned = psum.tile([P, PACK, P], F32, name="vs_turned", tag="turned", bufs=2)
-            for t in range(PACK):
-                nc.tensor.transpose(turned[:, t, :], vs_got[:, t:N:PACK], ident[:])
-            vs_cols = sb(f"vs_cols{b}", [P, PACK], F32)
-            nc.scalar.copy(out=vs_cols[:], in_=turned[:, :, 0])
+        def token_scales():
+            vs_got = sb("vs_got", [P, B * N], F32, tag="got0")
+            nc.vector.tensor_copy(vs_got[:], vs_pool[:].indirect(offsets[:]))
+            return vs_got
+
+        def spread_scales(vs_got):
+            vs_cols = sb("vs_cols", [P, B, 8], F32, tag="v_raw0")
+            for b in range(B):
+                nc.sync.dma_start(out=vs_cols[:, b, 0:PACK], in_=vs_got[0:1, b * N : (b + 1) * N])
             return vs_cols
 
         def gather_values(b):
             v_got = sb(f"v_got{b}", [P, N], U32)
             nc.vector.tensor_copy(v_got[:], v_pairs[:, 0 : 2 * (b + 1) * SEG].bitcast(U32).indirect(listed(b)))
-            turned = psum.tile([P, PACK, P], F32, name="v_turned", tag="turned", bufs=2)
+            turned = psum.tile([P, PACK, P], F32, name="v_turned", tag="turned", bufs=4)
             for t in range(PACK):
                 nc.tensor.transpose(turned[:, t, :], v_got[:].bitcast(F32)[:, t:N:PACK], ident[:])
-            v_woven = sb(f"v_woven{b}", [P, DV, PACK], BF16)
+            v_woven = sb(f"v_woven{b}", [P, DV, PACK], BF16, tag="ks_then_v" if b == 0 else "")
             nc.scalar.copy(out=v_woven[:], in_=turned[:].bitcast(BF16).rearrange("p t e -> p e t"))
             return v_woven
 
@@ -192,7 +197,7 @@ def tile_attend_soft_sink_gate_segb2q256n512t2048_kernel(
             nc.vector.tensor_tensor(
                 out=w_woven[:],
                 in0=turned[:].rearrange("p t q -> p q t"),
-                in1=vs_cols[:].unsqueeze(1).to_broadcast([P, P, PACK]),
+                in1=vs_cols[:, j // HALVES, 0:PACK].unsqueeze(1).to_broadcast([P, P, PACK]),
                 op=ALU.mult,
             )
             return w_woven
@@ -223,32 +228,20 @@ def tile_attend_soft_sink_gate_segb2q256n512t2048_kernel(
             b, h = divmod(j, HALVES)
             nc.sync.dma_start(out=out[b, h * P : (h + 1) * P, :], in_=result[:])
 
-        nc.scalar.activation(out=neg_logits[:, :, N], in_=sink_cols[:], func=ACT.Copy, scale=-1.0)
-        k_codes = [keys(b) for b in range(B)]
+        k_got = [gather_keys(b) for b in range(B)]
+        k_codes = [part_keys(b, k_got[b]) for b in range(B)]
+        vs_got = token_scales()
+        for b in range(B):
+            cast_values(b)
+        vs_cols = spread_scales(vs_got)
         accs = [scores(b, h, k_codes[b]) for b in range(B) for h in range(HALVES)]
-        cast_values(0)
-        soft = [softmax(j, accs[j]) for j in range(HALVES)]
-        vs_cols = [token_scales(0)]
-        cast_values(1)
-        v_woven = [gather_values(0)]
-        soft.append(softmax(2, accs[2]))
-        w_woven = [weigh(0, soft[0], vs_cols[0])]
-        soft.append(softmax(3, accs[3]))
-        w_woven.append(weigh(1, soft[1], vs_cols[0]))
-        vs_cols.append(token_scales(1))
-        v_mx = [quantize("v0", v_woven[0], DV)]
-        w_mx = [quantize(f"w{j}", w_woven[j], P) for j in range(HALVES)]
-        v_woven.append(gather_values(1))
-        mixed = [mix(w_mx[j], v_mx[0]) for j in range(HALVES)]
-        nc.scalar.activation(out=half_tanh[:], in_=og_sb[:].rearrange("p j e -> p (j e)"), func=ACT.Tanh, scale=0.5)
-        nc.gpsimd.tensor_scalar(out=gate[:], in0=half_tanh[:], scalar1=0.5, scalar2=0.5, op0=ALU.mult, op1=ALU.add)
-        w_woven.append(weigh(2, soft[2], vs_cols[1]))
-        w_woven.append(weigh(3, soft[3], vs_cols[1]))
+        v_woven = [gather_values(b) for b in range(B)]
+        soft = [softmax(j, accs[j]) for j in range(TILES)]
+        v_mx = [quantize(f"v{b}", v_woven[b], DV) for b in range(B)]
+        w_woven = [weigh(j, soft[j], vs_cols) for j in range(TILES)]
         nc.vector.reciprocal(inverses[:], totals[:])
-        finish(0, mixed[0])
-        v_mx.append(quantize("v1", v_woven[1], DV))
-        for j in range(HALVES, TILES):
-            w_mx.append(quantize(f"w{j}", w_woven[j], P))
-            mixed.append(mix(w_mx[j], v_mx[1]))
-        for j in range(1, TILES):
+        mixed = []
+        for j in range(TILES):
+            mixed.append(mix(quantize(f"w{j}", w_woven[j], P), v_mx[j // HALVES]))
+        for j in range(TILES):
             finish(j, mixed[j])

@@ -25,6 +25,9 @@ HALVES = NQ // P
 TILES = B * HALVES
 LIST_COLS = N // 16
 ROW = N + 8
+KS_ROW0 = 96
+V1_PARTS = 2
+V1_COLS = SEG // V1_PARTS
 
 
 def tile_attend_soft_sink_gate_segb2q256n512t2048_kernel(
@@ -33,6 +36,7 @@ def tile_attend_soft_sink_gate_segb2q256n512t2048_kernel(
     nc = tc.nc
     with ExitStack() as ctx:
         keep = ctx.enter_context(tc.tile_pool(name="keep", bufs=1))
+        shared = ctx.enter_context(tc.tile_pool(name="shared", bufs=1))
         psum = ctx.enter_context(tc.psum_pool(name="psum", bufs=1))
 
         def sb(name, shape, dtype, tag=""):
@@ -40,81 +44,108 @@ def tile_attend_soft_sink_gate_segb2q256n512t2048_kernel(
 
         offsets = keep.tile([P, B * LIST_COLS], U16, name="offsets")
         k_pool = sb("k_pool", [P, T], I32)
-        ks_pool = sb("ks_pool", [P, T], U8, tag="ks_then_v")
+        v1_bytes = 2 * V1_COLS * 4
+        ks_pool = shared.tile([P, T], U8, name="ks_pool", offset=v1_bytes - T // 2)
         vs_pool = sb("vs_pool", [P, T], F32)
-        v_pairs = sb("v_pairs", [P, 2 * T], BF16)
+        v_pool = sb("v_pool", [P, 2 * T], BF16)
         neg_logits = sb("neg_logits", [P, TILES, ROW], F32)
         q_planes = sb("q_planes", [P, B * PASSES * NQ], U8)
-        ks_got = sb("ks_got", [P, B * N], U8)
+        q_codes = sb("q_codes", [P, B * PASSES, NQ], I32)
+        ks_got = sb("ks_got", [P, B * N], U8, tag="ks_got_then_og")
         k_planes = sb("k_planes", [P, PASSES * B * N], U8)
-        sink_rows = sb("sink_rows", [P, P], F32)
-        og_sb = sb("og_sb", [P, TILES, DV], F32)
-        half_tanh = sb("half_tanh", [P, TILES * DV], F32, tag="tanh_then_q")
+        sink_sb = sb("sink_sb", [P, TILES], F32)
+        half_tanh = sb("half_tanh", [P, TILES * DV], F32)
         gate = sb("gate", [P, TILES * DV], F32)
         ident = sb("ident", [P, P], F32)
         totals = sb("totals", [P, TILES], F32)
         inverses = sb("inverses", [P, TILES], F32)
-        warm = sb("warm", [P, 2], F32)
+        v0_raw = [sb(f"v0_raw{h}", [P, SEG], F32) for h in range(2)]
 
-        nc.vector.memset(warm[:, 0:1], 0.0)
-        nc.vector.memset(ks_pool[32:64, :].bitcast(I32), 0)
-        nc.vector.memset(ks_pool[64:128, :].bitcast(I32), 0)
-        nc.vector.memset(sink_rows[:], 0.0)
+        nc.vector.memset(q_planes[:].bitcast(I32), 0)
+        nc.vector.memset(ks_pool[0:KS_ROW0, :].bitcast(I32), 0)
         nc.vector.memset(k_planes[:].bitcast(I32), 0)
-        make_identity(nc, ident[:])
         nc.gpsimd.memset(vs_pool[:], 0.0)
-        nc.gpsimd.memset(q_planes[:].bitcast(I32), 0)
+        make_identity(nc, ident[:])
 
         k_flat = k_words[0].rearrange("p t r -> p (t r)").bitcast(I32)
-        v_rows = vT.rearrange("(p h) t -> p h t", h=2)
 
-        nc.scalar.activation(out=warm[:, 1:2], in_=warm[:, 0:1], func=ACT.Exp)
         nc.sync.dma_start(offsets[:], offs)
-        nc.sync.dma_start(out=ks_pool[0:32, :].bitcast(I32), in_=k_scales.rearrange("o f t -> f o t").bitcast(I32))
-        nc.sync.dma_start(out=og_sb[:], in_=og.rearrange("b (h p) e -> p (b h) e", p=P))
-        nc.sync.dma_start(out=k_pool[:, 0:SEG], in_=k_flat[:, 0:SEG])
-        nc.sync.dma_start(out=k_pool[:, SEG:T], in_=k_flat[:, SEG:T])
-        v_raw = [sb("v_raw0", [P, 2, SEG], F32)]
-        nc.sync.dma_start(out=v_raw[0][:], in_=v_rows[:, :, 0:SEG])
-        nc.scalar.dma_start(out=sink_rows[0:TILES, :], in_=sink.rearrange("b (h p) one -> (b h) (p one)", p=P))
-        nc.scalar.dma_start(out=vs_pool[0:1, :], in_=vs[0:1, :])
-
-        def listed(b):
-            return offsets[:, b * LIST_COLS : (b + 1) * LIST_COLS]
-
-        nc.vector.tensor_copy(ks_got[:], ks_pool[:].indirect(offsets[:]))
-        v_raw.append(sb("v_raw1", [P, 2, SEG], F32, tag="ks_then_v"))
-        nc.sync.dma_start(out=v_raw[1][:], in_=v_rows[:, :, SEG:T])
-        for quad in range(4):
-            nc.sync.dma_start(
-                out=k_planes[32 * quad : 32 * quad + 4, :].bitcast(I32).rearrange("f (o n) -> f o n", o=PASSES),
-                in_=ks_got[8 * quad : 8 * quad + 8, :].bitcast(I32),
-            )
+        nc.sync.dma_start(
+            out=ks_pool[KS_ROW0:P, :].bitcast(I32), in_=k_scales.rearrange("o f t -> f o t").bitcast(I32)
+        )
+        for h in range(2):
+            nc.sync.dma_start(out=v0_raw[h][:], in_=vT[h * P : (h + 1) * P, 0:SEG])
         for quad in range(4):
             nc.sync.dma_start(
                 out=q_planes[32 * quad : 32 * quad + 4, :].bitcast(I32).rearrange("f (g q) -> f g q", g=B * PASSES),
                 in_=q_scales[:, :, 4 * quad : 4 * quad + 4, :].rearrange("b o f q -> f (b o) q").bitcast(I32),
             )
-        nc.scalar.activation(out=half_tanh[:], in_=og_sb[:].rearrange("p j e -> p (j e)"), func=ACT.Tanh, scale=0.5)
-        nc.scalar.activation(out=gate[:], in_=half_tanh[:], func=ACT.Copy, scale=0.5, bias=0.5)
-        q_codes = sb("q_codes", [P, B * PASSES, NQ], I32, tag="tanh_then_q")
+        for b in range(B):
+            nc.sync.dma_start(out=k_pool[:, b * SEG : (b + 1) * SEG], in_=k_flat[:, b * SEG : (b + 1) * SEG])
         nc.sync.dma_start(out=q_codes[:], in_=q_words.rearrange("b o p q r -> p (b o) (q r)").bitcast(I32))
-        sink_turned = psum.tile([P, P], F32, name="sink_turned", tag="turned", bufs=4)
-        nc.tensor.transpose(sink_turned[:], sink_rows[:], ident[:])
-        nc.scalar.activation(out=neg_logits[:, :, N], in_=sink_turned[:, 0:TILES], func=ACT.Copy, scale=-1.0)
+        nc.sync.dma_start(out=vs_pool[0:1, :], in_=vs[0:1, :])
+        with nc.allow_non_contiguous_dma(reason="one logit a query row"):
+            nc.sync.dma_start(out=sink_sb[:], in_=sink.rearrange("b (h p) one -> p (b h one)", p=P))
+
+        def listed(b):
+            return offsets[:, b * LIST_COLS : (b + 1) * LIST_COLS]
+
+        nc.vector.tensor_copy(ks_got[:], ks_pool[:].indirect(offsets[:]))
+        for quad in range(4):
+            nc.sync.dma_start(
+                out=k_planes[32 * quad : 32 * quad + 4, :].bitcast(I32).rearrange("f (o n) -> f o n", o=PASSES),
+                in_=ks_got[KS_ROW0 + 8 * quad : KS_ROW0 + 8 * quad + 8, :].bitcast(I32),
+            )
+        v_rows = vT.rearrange("(p h) t -> p h t", h=2)
+        v1_raw = []
+        for c in range(V1_PARTS):
+            part = shared.tile([P, 2, V1_COLS], F32, name=f"v1_raw{c}", offset=c * v1_bytes)
+            nc.sync.dma_start(out=part[:], in_=v_rows[:, :, SEG + c * V1_COLS : SEG + (c + 1) * V1_COLS])
+            v1_raw.append(part)
+        og_sb = sb("og_sb", [P, TILES, DV], F32, tag="ks_got_then_og")
+        nc.sync.dma_start(out=og_sb[:], in_=og.rearrange("b (h p) e -> p (b h) e", p=P))
+
+        def values_on_scalar():
+            for h in range(2):
+                nc.scalar.activation(out=v_pool[:, h * SEG : (h + 1) * SEG], in_=v0_raw[h][:], func=ACT.Copy)
+            got = []
+            for h in range(2):
+                v_got = sb(f"v0_got{h}", [P, 2, P, 2], BF16)
+                nc.scalar.activation(
+                    out=v_got[:].rearrange("p u s e -> p s u e"),
+                    in_=v_pool[:, h * SEG : (h + 1) * SEG].indirect(listed(0)),
+                    func=ACT.Copy,
+                )
+                got.append(v_got)
+            turned = psum.tile([P, 2, 2, P], F32, name="v0_turned", tag="turned", bufs=4)
+            for h in range(2):
+                words = got[h][:].rearrange("p u s e -> p (u s e)").bitcast(F32)
+                for u in range(2):
+                    nc.tensor.transpose(turned[:, h, u, :], words[:, u * P : (u + 1) * P], ident[:])
+            v_woven = sb("v_woven0", [P, DV, PACK], BF16)
+            nc.scalar.copy(
+                out=v_woven[:].rearrange("p e t -> p (e t)").bitcast(F32).rearrange("p (h e u) -> p h e u", h=2, u=2),
+                in_=turned[:].rearrange("p h u e -> p h e u"),
+            )
+            return v_woven
 
         def gather_keys(b):
-            k_got = sb(f"k_got{b}", [P, N], U32, tag=f"got{b}")
+            k_got = sb(f"k_got{b}", [P, N], U32)
             nc.vector.tensor_copy(k_got[:], k_pool[:, 0 : (b + 1) * SEG].bitcast(U32).indirect(listed(b)))
-            return k_got
-
-        def part_keys(b, k_got):
             k_codes = sb(f"k_codes{b}", [P, PASSES, 2 * N], U8)
             nc.vector.tensor_copy(
                 out=k_codes[:].bitcast(U16),
                 in_=k_got[:].bitcast(U16).rearrange("p (i o) -> p o i", o=PASSES),
             )
             return k_codes
+
+        def token_scales():
+            vs_got = sb("vs_got", [P, B * N], F32)
+            nc.vector.tensor_copy(vs_got[:], vs_pool[:].indirect(offsets[:]))
+            vs_cols = sb("vs_cols", [P, B, 8], F32)
+            for b in range(B):
+                nc.sync.dma_start(out=vs_cols[:, b, 0:PACK], in_=vs_got[0:1, b * N : (b + 1) * N])
+            return vs_cols
 
         def scores(b, h, k_codes):
             acc = psum.tile([P, N], F32, name="score", tag="acc", bufs=4)
@@ -132,7 +163,7 @@ def tile_attend_soft_sink_gate_segb2q256n512t2048_kernel(
             return acc
 
         def softmax(j, acc):
-            neg_max = sb(f"neg_max{j}", [P, 1], F32, tag="")
+            neg_max = sb(f"neg_max{j}", [P, 1], F32)
             nc.vector.tensor_scalar(
                 out=neg_logits[:, j, 0:N].rearrange("p (t s) -> p t s", t=PACK),
                 in0=acc[:].rearrange("p (s t) -> p t s", t=PACK),
@@ -156,31 +187,21 @@ def tile_attend_soft_sink_gate_segb2q256n512t2048_kernel(
                 nc.tensor.transpose(turned[:, t, :], probs[:, t * P : (t + 1) * P], ident[:])
             return turned
 
-        def cast_values(b):
+        def cast_pairs(c):
+            first = 2 * (SEG + c * V1_COLS)
             nc.scalar.activation(
-                out=v_pairs[:, 2 * b * SEG : 2 * (b + 1) * SEG].rearrange("p (t h) -> p t h", h=2),
-                in_=v_raw[b][:].rearrange("p h t -> p t h"),
+                out=v_pool[:, first : first + 2 * V1_COLS].rearrange("p (t h) -> p t h", h=2),
+                in_=v1_raw[c][:].rearrange("p h t -> p t h"),
                 func=ACT.Copy,
             )
 
-        def token_scales():
-            vs_got = sb("vs_got", [P, B * N], F32, tag="got0")
-            nc.vector.tensor_copy(vs_got[:], vs_pool[:].indirect(offsets[:]))
-            return vs_got
-
-        def spread_scales(vs_got):
-            vs_cols = sb("vs_cols", [P, B, 8], F32, tag="v_raw0")
-            for b in range(B):
-                nc.sync.dma_start(out=vs_cols[:, b, 0:PACK], in_=vs_got[0:1, b * N : (b + 1) * N])
-            return vs_cols
-
-        def gather_values(b):
-            v_got = sb(f"v_got{b}", [P, N], U32)
-            nc.vector.tensor_copy(v_got[:], v_pairs[:, 0 : 2 * (b + 1) * SEG].bitcast(U32).indirect(listed(b)))
-            turned = psum.tile([P, PACK, P], F32, name="v_turned", tag="turned", bufs=4)
+        def values_on_vector():
+            v_got = sb("v1_got", [P, N], U32)
+            nc.vector.tensor_copy(v_got[:], v_pool[:].bitcast(U32).indirect(listed(1)))
+            turned = psum.tile([P, PACK, P], F32, name="v1_turned", tag="turned", bufs=4)
             for t in range(PACK):
                 nc.tensor.transpose(turned[:, t, :], v_got[:].bitcast(F32)[:, t:N:PACK], ident[:])
-            v_woven = sb(f"v_woven{b}", [P, DV, PACK], BF16, tag="ks_then_v" if b == 0 else "")
+            v_woven = sb("v_woven1", [P, DV, PACK], BF16)
             nc.scalar.copy(out=v_woven[:], in_=turned[:].bitcast(BF16).rearrange("p t e -> p e t"))
             return v_woven
 
@@ -228,20 +249,23 @@ def tile_attend_soft_sink_gate_segb2q256n512t2048_kernel(
             b, h = divmod(j, HALVES)
             nc.sync.dma_start(out=out[b, h * P : (h + 1) * P, :], in_=result[:])
 
-        k_got = [gather_keys(b) for b in range(B)]
-        k_codes = [part_keys(b, k_got[b]) for b in range(B)]
-        vs_got = token_scales()
-        for b in range(B):
-            cast_values(b)
-        vs_cols = spread_scales(vs_got)
+        v_woven = [values_on_scalar()]
+        k_codes = [gather_keys(b) for b in range(B)]
+        vs_cols = token_scales()
+        nc.scalar.activation(out=neg_logits[:, :, N], in_=sink_sb[:], func=ACT.Copy, scale=-1.0)
         accs = [scores(b, h, k_codes[b]) for b in range(B) for h in range(HALVES)]
-        v_woven = [gather_values(b) for b in range(B)]
-        soft = [softmax(j, accs[j]) for j in range(TILES)]
-        v_mx = [quantize(f"v{b}", v_woven[b], DV) for b in range(B)]
-        w_woven = [weigh(j, soft[j], vs_cols) for j in range(TILES)]
+        for c in range(V1_PARTS):
+            cast_pairs(c)
+        soft = [softmax(j, accs[j]) for j in range(HALVES)]
+        v_woven.append(values_on_vector())
+        soft.extend(softmax(j, accs[j]) for j in range(HALVES, TILES))
+        nc.scalar.activation(out=half_tanh[:], in_=og_sb[:].rearrange("p j e -> p (j e)"), func=ACT.Tanh, scale=0.5)
+        nc.scalar.activation(out=gate[:], in_=half_tanh[:], func=ACT.Copy, scale=0.5, bias=0.5)
         nc.vector.reciprocal(inverses[:], totals[:])
-        mixed = []
-        for j in range(TILES):
-            mixed.append(mix(quantize(f"w{j}", w_woven[j], P), v_mx[j // HALVES]))
-        for j in range(TILES):
-            finish(j, mixed[j])
+        for b in range(B):
+            tiles = range(b * HALVES, (b + 1) * HALVES)
+            w_woven = [weigh(j, soft[j], vs_cols) for j in tiles]
+            v_mx = quantize(f"v{b}", v_woven[b], DV)
+            mixed = [mix(quantize(f"w{j}", w, P), v_mx) for j, w in zip(tiles, w_woven)]
+            for j, acc in zip(tiles, mixed):
+                finish(j, acc)

@@ -26,8 +26,7 @@ TILES = B * HALVES
 LIST_COLS = N // 16
 ROW = N + 8
 KS_ROW0 = 96
-V1_PARTS = 2
-V1_COLS = SEG // V1_PARTS
+PLANES = DV // P
 
 
 def tile_attend_soft_sink_gate_segb2q256n512t2048_kernel(
@@ -36,7 +35,6 @@ def tile_attend_soft_sink_gate_segb2q256n512t2048_kernel(
     nc = tc.nc
     with ExitStack() as ctx:
         keep = ctx.enter_context(tc.tile_pool(name="keep", bufs=1))
-        shared = ctx.enter_context(tc.tile_pool(name="shared", bufs=1))
         psum = ctx.enter_context(tc.psum_pool(name="psum", bufs=1))
 
         def sb(name, shape, dtype, tag=""):
@@ -44,14 +42,13 @@ def tile_attend_soft_sink_gate_segb2q256n512t2048_kernel(
 
         offsets = keep.tile([P, B * LIST_COLS], U16, name="offsets")
         k_pool = sb("k_pool", [P, T], I32)
-        v1_bytes = 2 * V1_COLS * 4
-        ks_pool = shared.tile([P, T], U8, name="ks_pool", offset=v1_bytes - T // 2)
+        ks_pool = sb("ks_pool", [P, T], U8)
         vs_pool = sb("vs_pool", [P, T], F32)
         v_pool = sb("v_pool", [P, 2 * T], BF16)
         neg_logits = sb("neg_logits", [P, TILES, ROW], F32)
         q_planes = sb("q_planes", [P, B * PASSES * NQ], U8)
         q_codes = sb("q_codes", [P, B * PASSES, NQ], I32)
-        ks_got = sb("ks_got", [P, B * N], U8, tag="ks_got_then_og")
+        ks_got = sb("ks_got", [P, B * N], U8)
         k_planes = sb("k_planes", [P, PASSES * B * N], U8)
         sink_sb = sb("sink_sb", [P, TILES], F32)
         half_tanh = sb("half_tanh", [P, TILES * DV], F32)
@@ -59,7 +56,6 @@ def tile_attend_soft_sink_gate_segb2q256n512t2048_kernel(
         ident = sb("ident", [P, P], F32)
         totals = sb("totals", [P, TILES], F32)
         inverses = sb("inverses", [P, TILES], F32)
-        v0_raw = [sb(f"v0_raw{h}", [P, SEG], F32) for h in range(2)]
 
         nc.vector.memset(q_planes[:].bitcast(I32), 0)
         nc.vector.memset(ks_pool[0:KS_ROW0, :].bitcast(I32), 0)
@@ -73,19 +69,25 @@ def tile_attend_soft_sink_gate_segb2q256n512t2048_kernel(
         nc.sync.dma_start(
             out=ks_pool[KS_ROW0:P, :].bitcast(I32), in_=k_scales.rearrange("o f t -> f o t").bitcast(I32)
         )
-        for h in range(2):
-            nc.sync.dma_start(out=v0_raw[h][:], in_=vT[h * P : (h + 1) * P, 0:SEG])
+        v_raw = {}
+
+        def load_values(b, h, tag=""):
+            v_raw[b, h] = sb(f"v_raw{b}{h}", [P, SEG], F32, tag=tag)
+            nc.sync.dma_start(out=v_raw[b, h][:], in_=vT[h * P : (h + 1) * P, b * SEG : (b + 1) * SEG])
+
+        def load_keys(b):
+            nc.sync.dma_start(out=k_pool[:, b * SEG : (b + 1) * SEG], in_=k_flat[:, b * SEG : (b + 1) * SEG])
+
+        load_values(0, 0)
+        load_keys(0)
         for quad in range(4):
             nc.sync.dma_start(
                 out=q_planes[32 * quad : 32 * quad + 4, :].bitcast(I32).rearrange("f (g q) -> f g q", g=B * PASSES),
                 in_=q_scales[:, :, 4 * quad : 4 * quad + 4, :].rearrange("b o f q -> f (b o) q").bitcast(I32),
             )
-        for b in range(B):
-            nc.sync.dma_start(out=k_pool[:, b * SEG : (b + 1) * SEG], in_=k_flat[:, b * SEG : (b + 1) * SEG])
-        nc.sync.dma_start(out=q_codes[:], in_=q_words.rearrange("b o p q r -> p (b o) (q r)").bitcast(I32))
+        load_values(0, 1)
+        load_keys(1)
         nc.sync.dma_start(out=vs_pool[0:1, :], in_=vs[0:1, :])
-        with nc.allow_non_contiguous_dma(reason="one logit a query row"):
-            nc.sync.dma_start(out=sink_sb[:], in_=sink.rearrange("b (h p) one -> p (b h one)", p=P))
 
         def listed(b):
             return offsets[:, b * LIST_COLS : (b + 1) * LIST_COLS]
@@ -96,33 +98,32 @@ def tile_attend_soft_sink_gate_segb2q256n512t2048_kernel(
                 out=k_planes[32 * quad : 32 * quad + 4, :].bitcast(I32).rearrange("f (o n) -> f o n", o=PASSES),
                 in_=ks_got[KS_ROW0 + 8 * quad : KS_ROW0 + 8 * quad + 8, :].bitcast(I32),
             )
-        v_rows = vT.rearrange("(p h) t -> p h t", h=2)
-        v1_raw = []
-        for c in range(V1_PARTS):
-            part = shared.tile([P, 2, V1_COLS], F32, name=f"v1_raw{c}", offset=c * v1_bytes)
-            nc.sync.dma_start(out=part[:], in_=v_rows[:, :, SEG + c * V1_COLS : SEG + (c + 1) * V1_COLS])
-            v1_raw.append(part)
-        og_sb = sb("og_sb", [P, TILES, DV], F32, tag="ks_got_then_og")
+        load_values(1, 0)
+        nc.sync.dma_start(out=q_codes[:], in_=q_words.rearrange("b o p q r -> p (b o) (q r)").bitcast(I32))
+        load_values(1, 1)
+        with nc.allow_non_contiguous_dma(reason="one logit a query row"):
+            nc.sync.dma_start(out=sink_sb[:], in_=sink.rearrange("b (h p) one -> p (b h one)", p=P))
+        og_sb = sb("og_sb", [P, TILES, DV], F32)
         nc.sync.dma_start(out=og_sb[:], in_=og.rearrange("b (h p) e -> p (b h) e", p=P))
 
-        def values_on_scalar():
-            for h in range(2):
-                nc.scalar.activation(out=v_pool[:, h * SEG : (h + 1) * SEG], in_=v0_raw[h][:], func=ACT.Copy)
-            got = []
-            for h in range(2):
-                v_got = sb(f"v0_got{h}", [P, 2, P, 2], BF16)
-                nc.scalar.activation(
-                    out=v_got[:].rearrange("p u s e -> p s u e"),
-                    in_=v_pool[:, h * SEG : (h + 1) * SEG].indirect(listed(0)),
-                    func=ACT.Copy,
-                )
-                got.append(v_got)
-            turned = psum.tile([P, 2, 2, P], F32, name="v0_turned", tag="turned", bufs=4)
-            for h in range(2):
+        def gather_values(b, h):
+            plane = b * PLANES + h
+            nc.scalar.activation(out=v_pool[:, plane * SEG : (plane + 1) * SEG], in_=v_raw[b, h][:], func=ACT.Copy)
+            v_got = sb(f"v_got{b}{h}", [P, 2, P, 2], BF16)
+            nc.scalar.activation(
+                out=v_got[:].rearrange("p u s e -> p s u e"),
+                in_=v_pool[:, (plane - b) * SEG : (plane + 1) * SEG].indirect(listed(b)),
+                func=ACT.Copy,
+            )
+            return v_got
+
+        def turn_values(b, got):
+            turned = psum.tile([P, PLANES, 2, P], F32, name="v_turned", tag="acc", bufs=4)
+            for h in range(PLANES):
                 words = got[h][:].rearrange("p u s e -> p (u s e)").bitcast(F32)
                 for u in range(2):
                     nc.tensor.transpose(turned[:, h, u, :], words[:, u * P : (u + 1) * P], ident[:])
-            v_woven = sb("v_woven0", [P, DV, PACK], BF16)
+            v_woven = sb(f"v_woven{b}", [P, DV, PACK], BF16)
             nc.scalar.copy(
                 out=v_woven[:].rearrange("p e t -> p (e t)").bitcast(F32).rearrange("p (h e u) -> p h e u", h=2, u=2),
                 in_=turned[:].rearrange("p h u e -> p h e u"),
@@ -187,24 +188,6 @@ def tile_attend_soft_sink_gate_segb2q256n512t2048_kernel(
                 nc.tensor.transpose(turned[:, t, :], probs[:, t * P : (t + 1) * P], ident[:])
             return turned
 
-        def cast_pairs(c):
-            first = 2 * (SEG + c * V1_COLS)
-            nc.scalar.activation(
-                out=v_pool[:, first : first + 2 * V1_COLS].rearrange("p (t h) -> p t h", h=2),
-                in_=v1_raw[c][:].rearrange("p h t -> p t h"),
-                func=ACT.Copy,
-            )
-
-        def values_on_vector():
-            v_got = sb("v1_got", [P, N], U32)
-            nc.vector.tensor_copy(v_got[:], v_pool[:].bitcast(U32).indirect(listed(1)))
-            turned = psum.tile([P, PACK, P], F32, name="v1_turned", tag="turned", bufs=4)
-            for t in range(PACK):
-                nc.tensor.transpose(turned[:, t, :], v_got[:].bitcast(F32)[:, t:N:PACK], ident[:])
-            v_woven = sb("v_woven1", [P, DV, PACK], BF16)
-            nc.scalar.copy(out=v_woven[:], in_=turned[:].bitcast(BF16).rearrange("p t e -> p e t"))
-            return v_woven
-
         def quantize(name, woven, cols):
             codes = sb(f"{name}_codes", [P, cols], U32)
             plane = sb(f"{name}_plane", [P, cols], U8)
@@ -249,18 +232,28 @@ def tile_attend_soft_sink_gate_segb2q256n512t2048_kernel(
             b, h = divmod(j, HALVES)
             nc.sync.dma_start(out=out[b, h * P : (h + 1) * P, :], in_=result[:])
 
-        v_woven = [values_on_scalar()]
+        def make_gate(j):
+            cols = slice(j * DV, (j + 1) * DV)
+            nc.scalar.activation(
+                out=half_tanh[:, cols], in_=og_sb[:].rearrange("p j e -> p (j e)")[:, cols], func=ACT.Tanh, scale=0.5
+            )
+            nc.gpsimd.tensor_scalar(
+                out=gate[:, cols], in0=half_tanh[:, cols], scalar1=0.5, scalar2=0.5, op0=ALU.mult, op1=ALU.add
+            )
+
+        v_got = [[gather_values(b, h) for h in range(PLANES)] for b in range(B)]
         k_codes = [gather_keys(b) for b in range(B)]
         vs_cols = token_scales()
-        nc.scalar.activation(out=neg_logits[:, :, N], in_=sink_sb[:], func=ACT.Copy, scale=-1.0)
+        nc.gpsimd.tensor_scalar(
+            out=neg_logits[:, :, N], in0=sink_sb[:], scalar1=-1.0, scalar2=0.0, op0=ALU.mult, op1=ALU.add
+        )
         accs = [scores(b, h, k_codes[b]) for b in range(B) for h in range(HALVES)]
-        for c in range(V1_PARTS):
-            cast_pairs(c)
-        soft = [softmax(j, accs[j]) for j in range(HALVES)]
-        v_woven.append(values_on_vector())
-        soft.extend(softmax(j, accs[j]) for j in range(HALVES, TILES))
-        nc.scalar.activation(out=half_tanh[:], in_=og_sb[:].rearrange("p j e -> p (j e)"), func=ACT.Tanh, scale=0.5)
-        nc.scalar.activation(out=gate[:], in_=half_tanh[:], func=ACT.Copy, scale=0.5, bias=0.5)
+        soft = [softmax(j, accs[j]) for j in range(TILES)]
+        v_woven = []
+        for b in range(B):
+            v_woven.append(turn_values(b, v_got[b]))
+            for j in range(b * HALVES, (b + 1) * HALVES):
+                make_gate(j)
         nc.vector.reciprocal(inverses[:], totals[:])
         for b in range(B):
             tiles = range(b * HALVES, (b + 1) * HALVES)

@@ -50,17 +50,18 @@ def tile_attend_soft_sink_gate_segb2q256n512t2048_kernel(
         q_codes = sb("q_codes", [P, B * PASSES, NQ], I32)
         ks_got = sb("ks_got", [P, B * N], U8)
         k_planes = sb("k_planes", [P, PASSES * B * N], U8)
-        sink_sb = sb("sink_sb", [P, TILES], F32)
+        sink_rows = sb("sink_rows", [P, P], F32)
         half_tanh = sb("half_tanh", [P, TILES * DV], F32)
         gate = sb("gate", [P, TILES * DV], F32)
         ident = sb("ident", [P, P], F32)
         totals = sb("totals", [P, TILES], F32)
         inverses = sb("inverses", [P, TILES], F32)
 
+        nc.vector.memset(sink_rows[:], 0.0)
         nc.vector.memset(q_planes[:].bitcast(I32), 0)
         nc.vector.memset(ks_pool[0:KS_ROW0, :].bitcast(I32), 0)
         nc.vector.memset(k_planes[:].bitcast(I32), 0)
-        nc.gpsimd.memset(vs_pool[:], 0.0)
+        nc.vector.memset(vs_pool[:].bitcast(I32), 0)
         make_identity(nc, ident[:])
 
         k_flat = k_words[0].rearrange("p t r -> p (t r)").bitcast(I32)
@@ -80,6 +81,7 @@ def tile_attend_soft_sink_gate_segb2q256n512t2048_kernel(
 
         load_values(0, 0)
         load_keys(0)
+        nc.sync.dma_start(out=sink_rows[0:TILES, :], in_=sink.rearrange("b (h p) one -> (b h) (p one)", p=P))
         for quad in range(4):
             nc.sync.dma_start(
                 out=q_planes[32 * quad : 32 * quad + 4, :].bitcast(I32).rearrange("f (g q) -> f g q", g=B * PASSES),
@@ -101,8 +103,6 @@ def tile_attend_soft_sink_gate_segb2q256n512t2048_kernel(
         load_values(1, 0)
         nc.sync.dma_start(out=q_codes[:], in_=q_words.rearrange("b o p q r -> p (b o) (q r)").bitcast(I32))
         load_values(1, 1)
-        with nc.allow_non_contiguous_dma(reason="one logit a query row"):
-            nc.sync.dma_start(out=sink_sb[:], in_=sink.rearrange("b (h p) one -> p (b h one)", p=P))
         og_sb = sb("og_sb", [P, TILES, DV], F32)
         nc.sync.dma_start(out=og_sb[:], in_=og.rearrange("b (h p) e -> p (b h) e", p=P))
 
@@ -244,9 +244,9 @@ def tile_attend_soft_sink_gate_segb2q256n512t2048_kernel(
         v_got = [[gather_values(b, h) for h in range(PLANES)] for b in range(B)]
         k_codes = [gather_keys(b) for b in range(B)]
         vs_cols = token_scales()
-        nc.gpsimd.tensor_scalar(
-            out=neg_logits[:, :, N], in0=sink_sb[:], scalar1=-1.0, scalar2=0.0, op0=ALU.mult, op1=ALU.add
-        )
+        sink_turned = psum.tile([P, P], F32, name="sink_turned", tag="turned", bufs=4)
+        nc.tensor.transpose(sink_turned[:], sink_rows[:], ident[:])
+        nc.scalar.activation(out=neg_logits[:, :, N], in_=sink_turned[:, 0:TILES], func=ACT.Copy, scale=-1.0)
         accs = [scores(b, h, k_codes[b]) for b in range(B) for h in range(HALVES)]
         soft = [softmax(j, accs[j]) for j in range(TILES)]
         v_woven = []

@@ -49,19 +49,16 @@ def tile_attend_soft_sink_gate_segb2q256n512t2048_kernel(
         q_planes = sb("q_planes", [P, B * PASSES * NQ], U8)
         q_codes = sb("q_codes", [P, B * PASSES, NQ], I32)
         ks_got = sb("ks_got", [P, B * N], U8)
-        k_planes = sb("k_planes", [P, PASSES * B * N], U8)
         sink_rows = sb("sink_rows", [P, P], F32)
-        half_tanh = sb("half_tanh", [P, TILES * DV], F32)
         gate = sb("gate", [P, TILES * DV], F32)
         ident = sb("ident", [P, P], F32)
         totals = sb("totals", [P, TILES], F32)
         inverses = sb("inverses", [P, TILES], F32)
 
         nc.vector.memset(sink_rows[:], 0.0)
-        nc.vector.memset(q_planes[:].bitcast(I32), 0)
+        nc.vector.memset(vs_pool[:, 0:SEG].bitcast(I32), 0)
+        nc.gpsimd.memset(vs_pool[:, SEG:T].bitcast(I32), 0)
         nc.vector.memset(ks_pool[0:KS_ROW0, :].bitcast(I32), 0)
-        nc.vector.memset(k_planes[:].bitcast(I32), 0)
-        nc.vector.memset(vs_pool[:].bitcast(I32), 0)
         make_identity(nc, ident[:])
 
         k_flat = k_words[0].rearrange("p t r -> p (t r)").bitcast(I32)
@@ -79,36 +76,40 @@ def tile_attend_soft_sink_gate_segb2q256n512t2048_kernel(
         def load_keys(b):
             nc.sync.dma_start(out=k_pool[:, b * SEG : (b + 1) * SEG], in_=k_flat[:, b * SEG : (b + 1) * SEG])
 
-        load_values(0, 0)
-        load_keys(0)
-        nc.sync.dma_start(out=sink_rows[0:TILES, :], in_=sink.rearrange("b (h p) one -> (b h) (p one)", p=P))
         for quad in range(4):
-            nc.sync.dma_start(
+            nc.scalar.dma_start(
                 out=q_planes[32 * quad : 32 * quad + 4, :].bitcast(I32).rearrange("f (g q) -> f g q", g=B * PASSES),
                 in_=q_scales[:, :, 4 * quad : 4 * quad + 4, :].rearrange("b o f q -> f (b o) q").bitcast(I32),
             )
-        load_values(0, 1)
-        load_keys(1)
+        load_values(0, 0)
+        load_keys(0)
         nc.sync.dma_start(out=vs_pool[0:1, :], in_=vs[0:1, :])
+        load_values(0, 1)
+        load_values(1, 0)
+        load_keys(1)
+        nc.sync.dma_start(out=q_codes[:], in_=q_words.rearrange("b o p q r -> p (b o) (q r)").bitcast(I32))
+        nc.sync.dma_start(out=sink_rows[0:TILES, :], in_=sink.rearrange("b (h p) one -> (b h) (p one)", p=P))
 
         def listed(b):
             return offsets[:, b * LIST_COLS : (b + 1) * LIST_COLS]
 
         nc.vector.tensor_copy(ks_got[:], ks_pool[:].indirect(offsets[:]))
+        k_planes = sb("k_planes", [P, PASSES * B * N], U8)
         for quad in range(4):
             nc.sync.dma_start(
                 out=k_planes[32 * quad : 32 * quad + 4, :].bitcast(I32).rearrange("f (o n) -> f o n", o=PASSES),
                 in_=ks_got[KS_ROW0 + 8 * quad : KS_ROW0 + 8 * quad + 8, :].bitcast(I32),
             )
-        load_values(1, 0)
-        nc.sync.dma_start(out=q_codes[:], in_=q_words.rearrange("b o p q r -> p (b o) (q r)").bitcast(I32))
         load_values(1, 1)
         og_sb = sb("og_sb", [P, TILES, DV], F32)
         nc.sync.dma_start(out=og_sb[:], in_=og.rearrange("b (h p) e -> p (b h) e", p=P))
 
-        def gather_values(b, h):
+        def cast_values(b, h):
             plane = b * PLANES + h
             nc.scalar.activation(out=v_pool[:, plane * SEG : (plane + 1) * SEG], in_=v_raw[b, h][:], func=ACT.Copy)
+
+        def gather_values(b, h):
+            plane = b * PLANES + h
             v_got = sb(f"v_got{b}{h}", [P, 2, P, 2], BF16)
             nc.scalar.activation(
                 out=v_got[:].rearrange("p u s e -> p s u e"),
@@ -118,7 +119,7 @@ def tile_attend_soft_sink_gate_segb2q256n512t2048_kernel(
             return v_got
 
         def turn_values(b, got):
-            turned = psum.tile([P, PLANES, 2, P], F32, name="v_turned", tag="acc", bufs=4)
+            turned = psum.tile([P, PLANES, 2, P], F32, name="v_turned", tag=f"bank{b}")
             for h in range(PLANES):
                 words = got[h][:].rearrange("p u s e -> p (u s e)").bitcast(F32)
                 for u in range(2):
@@ -130,9 +131,14 @@ def tile_attend_soft_sink_gate_segb2q256n512t2048_kernel(
             )
             return v_woven
 
+        vs_cols = sb("vs_cols", [P, B, 8], F32)
+
         def gather_keys(b):
             k_got = sb(f"k_got{b}", [P, N], U32)
             nc.vector.tensor_copy(k_got[:], k_pool[:, 0 : (b + 1) * SEG].bitcast(U32).indirect(listed(b)))
+            vs_got = sb(f"vs_got{b}", [P, N], F32)
+            nc.vector.tensor_copy(vs_got[:], vs_pool[:, 0 : (b + 1) * SEG].indirect(listed(b)))
+            nc.sync.dma_start(out=vs_cols[:, b, 0:PACK], in_=vs_got[0:1, :])
             k_codes = sb(f"k_codes{b}", [P, PASSES, 2 * N], U8)
             nc.vector.tensor_copy(
                 out=k_codes[:].bitcast(U16),
@@ -140,16 +146,8 @@ def tile_attend_soft_sink_gate_segb2q256n512t2048_kernel(
             )
             return k_codes
 
-        def token_scales():
-            vs_got = sb("vs_got", [P, B * N], F32)
-            nc.vector.tensor_copy(vs_got[:], vs_pool[:].indirect(offsets[:]))
-            vs_cols = sb("vs_cols", [P, B, 8], F32)
-            for b in range(B):
-                nc.sync.dma_start(out=vs_cols[:, b, 0:PACK], in_=vs_got[0:1, b * N : (b + 1) * N])
-            return vs_cols
-
         def scores(b, h, k_codes):
-            acc = psum.tile([P, N], F32, name="score", tag="acc", bufs=4)
+            acc = psum.tile([P, N], F32, name="score", tag=f"bank{b * HALVES + h}")
             for o in range(PASSES):
                 first = (b * PASSES + o) * NQ + h * P
                 nc.tensor.matmul_mx(
@@ -166,8 +164,8 @@ def tile_attend_soft_sink_gate_segb2q256n512t2048_kernel(
         def softmax(j, acc):
             neg_max = sb(f"neg_max{j}", [P, 1], F32)
             nc.vector.tensor_scalar(
-                out=neg_logits[:, j, 0:N].rearrange("p (t s) -> p t s", t=PACK),
-                in0=acc[:].rearrange("p (s t) -> p t s", t=PACK),
+                out=neg_logits[:, j, 0:N].rearrange("p (t s) -> p s t", t=PACK),
+                in0=acc[:].rearrange("p (s t) -> p s t", t=PACK),
                 scalar1=-1.0,
                 scalar2=neg_logits[:, j, N : N + 1],
                 op0=ALU.mult,
@@ -183,13 +181,13 @@ def tile_attend_soft_sink_gate_segb2q256n512t2048_kernel(
                 scale=-1.0,
                 accum_out=totals[:, j : j + 1],
             )
-            turned = psum.tile([P, PACK, P], F32, name="probs_turned", tag="turned", bufs=4)
+            turned = psum.tile([P, PACK, P], F32, name="probs_turned", tag=f"bank{4 + j}")
             for t in range(PACK):
                 nc.tensor.transpose(turned[:, t, :], probs[:, t * P : (t + 1) * P], ident[:])
             return turned
 
-        def quantize(name, woven, cols):
-            codes = sb(f"{name}_codes", [P, cols], U32)
+        def quantize(name, woven, cols, tag=""):
+            codes = sb(f"{name}_codes", [P, cols], U32, tag=tag)
             plane = sb(f"{name}_plane", [P, cols], U8)
             nc.vector.quantize_mx(
                 out=codes[:].bitcast(FP8X4), scales=plane[:], in_=woven[:].rearrange("p c t -> p (c t)")
@@ -206,8 +204,8 @@ def tile_attend_soft_sink_gate_segb2q256n512t2048_kernel(
             )
             return w_woven
 
-        def mix(w_mx, v_mx):
-            acc = psum.tile([P, DV], F32, name="mixed", tag="acc", bufs=4)
+        def mix(j, w_mx, v_mx):
+            acc = psum.tile([P, DV], F32, name="mixed", tag=f"bank{(j + 2) % TILES}")
             nc.tensor.matmul_mx(
                 out=acc[:],
                 lhsT=w_mx[0][:].bitcast(FP8X4),
@@ -241,24 +239,31 @@ def tile_attend_soft_sink_gate_segb2q256n512t2048_kernel(
                 out=gate[:, cols], in0=half_tanh[:, cols], scalar1=0.5, scalar2=0.5, op0=ALU.mult, op1=ALU.add
             )
 
-        v_got = [[gather_values(b, h) for h in range(PLANES)] for b in range(B)]
+        v_got = {}
+        for h in range(PLANES):
+            cast_values(0, h)
+            v_got[0, h] = gather_values(0, h)
         k_codes = [gather_keys(b) for b in range(B)]
-        vs_cols = token_scales()
-        sink_turned = psum.tile([P, P], F32, name="sink_turned", tag="turned", bufs=4)
+        accs = [scores(b, h, k_codes[b]) for b in range(B) for h in range(HALVES)]
+        cast_values(1, 0)
+        v_got[1, 0] = gather_values(1, 0)
+        sink_turned = psum.tile([P, P], F32, name="sink_turned", tag="bank4")
         nc.tensor.transpose(sink_turned[:], sink_rows[:], ident[:])
         nc.scalar.activation(out=neg_logits[:, :, N], in_=sink_turned[:, 0:TILES], func=ACT.Copy, scale=-1.0)
-        accs = [scores(b, h, k_codes[b]) for b in range(B) for h in range(HALVES)]
+        cast_values(1, 1)
         soft = [softmax(j, accs[j]) for j in range(TILES)]
-        v_woven = []
-        for b in range(B):
-            v_woven.append(turn_values(b, v_got[b]))
-            for j in range(b * HALVES, (b + 1) * HALVES):
-                make_gate(j)
+        v_woven = [turn_values(0, [v_got[0, h] for h in range(PLANES)])]
+        v_got[1, 1] = gather_values(1, 1)
+        half_tanh = sb("half_tanh", [P, TILES * DV], F32, tag="neg_logits")
+        for j in range(HALVES):
+            make_gate(j)
+        v_woven.append(turn_values(1, [v_got[1, h] for h in range(PLANES)]))
+        for j in range(HALVES, TILES):
+            make_gate(j)
         nc.vector.reciprocal(inverses[:], totals[:])
-        for b in range(B):
-            tiles = range(b * HALVES, (b + 1) * HALVES)
-            w_woven = [weigh(j, soft[j], vs_cols) for j in tiles]
-            v_mx = quantize(f"v{b}", v_woven[b], DV)
-            mixed = [mix(quantize(f"w{j}", w, P), v_mx) for j, w in zip(tiles, w_woven)]
-            for j, acc in zip(tiles, mixed):
-                finish(j, acc)
+        w_woven = [weigh(j, soft[j], vs_cols) for j in range(TILES)]
+        w_mx = [quantize(f"w{j}", w_woven[j], P) for j in range(TILES)]
+        v_mx = [quantize(f"v{b}", v_woven[b], DV) for b in range(B)]
+        mixed = [mix(j, w_mx[j], v_mx[j // HALVES]) for j in range(TILES)]
+        for j in range(TILES):
+            finish(j, mixed[j])

@@ -84,11 +84,11 @@ def tile_attend_soft_sink_gate_segb2q256n512t2048_kernel(
         load_values(0, 0)
         load_keys(0)
         nc.sync.dma_start(out=vs_pool[0:1, :], in_=vs[0:1, :])
-        load_values(0, 1)
-        load_values(1, 0)
-        load_keys(1)
-        nc.sync.dma_start(out=q_codes[:], in_=q_words.rearrange("b o p q r -> p (b o) (q r)").bitcast(I32))
         nc.sync.dma_start(out=sink_rows[0:TILES, :], in_=sink.rearrange("b (h p) one -> (b h) (p one)", p=P))
+        load_values(0, 1)
+        load_keys(1)
+        load_values(1, 0)
+        nc.sync.dma_start(out=q_codes[:], in_=q_words.rearrange("b o p q r -> p (b o) (q r)").bitcast(I32))
 
         def listed(b):
             return offsets[:, b * LIST_COLS : (b + 1) * LIST_COLS]
@@ -118,15 +118,16 @@ def tile_attend_soft_sink_gate_segb2q256n512t2048_kernel(
             )
             return v_got
 
-        def turn_values(b, got):
-            turned = psum.tile([P, PLANES, 2, P], F32, name="v_turned", tag=f"bank{b}")
-            for h in range(PLANES):
+        def turn_values(name, got, bank):
+            count = len(got)
+            turned = psum.tile([P, count, 2, P], F32, name="v_turned", tag=f"bank{bank}")
+            for h in range(count):
                 words = got[h][:].rearrange("p u s e -> p (u s e)").bitcast(F32)
                 for u in range(2):
                     nc.tensor.transpose(turned[:, h, u, :], words[:, u * P : (u + 1) * P], ident[:])
-            v_woven = sb(f"v_woven{b}", [P, DV, PACK], BF16)
+            v_woven = sb(name, [P, count * P, PACK], BF16)
             nc.scalar.copy(
-                out=v_woven[:].rearrange("p e t -> p (e t)").bitcast(F32).rearrange("p (h e u) -> p h e u", h=2, u=2),
+                out=v_woven[:].rearrange("p e t -> p (e t)").bitcast(F32).rearrange("p (h e u) -> p h e u", h=count, u=2),
                 in_=turned[:].rearrange("p h u e -> p h e u"),
             )
             return v_woven
@@ -195,30 +196,32 @@ def tile_attend_soft_sink_gate_segb2q256n512t2048_kernel(
             return codes, plane
 
         def weigh(j, turned, vs_cols):
-            w_woven = sb(f"w_woven{j}", [P, P, PACK], BF16)
+            b, h = divmod(j, HALVES)
             nc.vector.tensor_tensor(
-                out=w_woven[:],
+                out=w_woven[b][:, h * P : (h + 1) * P, :],
                 in0=turned[:].rearrange("p t q -> p q t"),
                 in1=vs_cols[:, j // HALVES, 0:PACK].unsqueeze(1).to_broadcast([P, P, PACK]),
                 op=ALU.mult,
             )
-            return w_woven
 
-        def mix(j, w_mx, v_mx):
+        def mix(j, w_mx, v_parts):
+            rows = slice(j % HALVES * P, (j % HALVES + 1) * P)
             acc = psum.tile([P, DV], F32, name="mixed", tag=f"bank{(j + 2) % TILES}")
-            nc.tensor.matmul_mx(
-                out=acc[:],
-                lhsT=w_mx[0][:].bitcast(FP8X4),
-                lhsT_scale=w_mx[1][:],
-                rhs=v_mx[0][:].bitcast(FP8X4),
-                rhs_scale=v_mx[1][:],
-                start=True,
-                stop=True,
-            )
+            width = DV // len(v_parts)
+            for c, v_mx in enumerate(v_parts):
+                nc.tensor.matmul_mx(
+                    out=acc[:, c * width : (c + 1) * width],
+                    lhsT=w_mx[0][:, rows].bitcast(FP8X4),
+                    lhsT_scale=w_mx[1][:, rows],
+                    rhs=v_mx[0][:].bitcast(FP8X4),
+                    rhs_scale=v_mx[1][:],
+                    start=True,
+                    stop=True,
+                )
             return acc
 
         def finish(j, acc):
-            result = sb(f"result{j}", [P, DV], F32)
+            result = sb(f"result{j}", [P, DV], F32, tag="v_woven11" if j == 0 else "")
             nc.vector.scalar_tensor_tensor(
                 out=result[:],
                 in0=acc[:],
@@ -230,40 +233,46 @@ def tile_attend_soft_sink_gate_segb2q256n512t2048_kernel(
             b, h = divmod(j, HALVES)
             nc.sync.dma_start(out=out[b, h * P : (h + 1) * P, :], in_=result[:])
 
-        def make_gate(j):
-            cols = slice(j * DV, (j + 1) * DV)
-            nc.scalar.activation(
-                out=half_tanh[:, cols], in_=og_sb[:].rearrange("p j e -> p (j e)")[:, cols], func=ACT.Tanh, scale=0.5
-            )
-            nc.gpsimd.tensor_scalar(
-                out=gate[:, cols], in0=half_tanh[:, cols], scalar1=0.5, scalar2=0.5, op0=ALU.mult, op1=ALU.add
-            )
+        def make_gate(tiles, tag):
+            half_tanh = sb(f"half_tanh{tiles[0]}", [P, len(tiles), DV], F32, tag=tag)
+            for c, j in enumerate(tiles):
+                nc.scalar.activation(out=half_tanh[:, c, :], in_=og_sb[:, j, :], func=ACT.Tanh, scale=0.5)
+                cols = slice(j * DV, (j + 1) * DV)
+                if j < TILES - 1:
+                    nc.gpsimd.tensor_scalar(
+                        out=gate[:, cols], in0=half_tanh[:, c, :], scalar1=0.5, scalar2=0.5, op0=ALU.mult, op1=ALU.add
+                    )
+                else:
+                    nc.scalar.activation(out=gate[:, cols], in_=half_tanh[:, c, :], func=ACT.Copy, scale=0.5, bias=0.5)
 
         v_got = {}
         for h in range(PLANES):
             cast_values(0, h)
             v_got[0, h] = gather_values(0, h)
+        sink_turned = psum.tile([P, P], F32, name="sink_turned", tag="bank4")
+        nc.tensor.transpose(sink_turned[:], sink_rows[:], ident[:])
+        nc.scalar.activation(out=neg_logits[:, :, N], in_=sink_turned[:, 0:TILES], func=ACT.Copy, scale=-1.0)
         k_codes = [gather_keys(b) for b in range(B)]
         accs = [scores(b, h, k_codes[b]) for b in range(B) for h in range(HALVES)]
         cast_values(1, 0)
         v_got[1, 0] = gather_values(1, 0)
-        sink_turned = psum.tile([P, P], F32, name="sink_turned", tag="bank4")
-        nc.tensor.transpose(sink_turned[:], sink_rows[:], ident[:])
-        nc.scalar.activation(out=neg_logits[:, :, N], in_=sink_turned[:, 0:TILES], func=ACT.Copy, scale=-1.0)
         cast_values(1, 1)
         soft = [softmax(j, accs[j]) for j in range(TILES)]
-        v_woven = [turn_values(0, [v_got[0, h] for h in range(PLANES)])]
+        first_woven = turn_values("v_woven0", [v_got[0, h] for h in range(PLANES)], 0)
+        second_woven = [turn_values("v_woven10", [v_got[1, 0]], 1)]
         v_got[1, 1] = gather_values(1, 1)
-        half_tanh = sb("half_tanh", [P, TILES * DV], F32, tag="neg_logits")
-        for j in range(HALVES):
-            make_gate(j)
-        v_woven.append(turn_values(1, [v_got[1, h] for h in range(PLANES)]))
-        for j in range(HALVES, TILES):
-            make_gate(j)
+        make_gate(range(TILES - 1), tag="neg_logits")
+        second_woven.append(turn_values("v_woven11", [v_got[1, 1]], 4))
+        make_gate(range(TILES - 1, TILES), tag="v_got11")
         nc.vector.reciprocal(inverses[:], totals[:])
-        w_woven = [weigh(j, soft[j], vs_cols) for j in range(TILES)]
-        w_mx = [quantize(f"w{j}", w_woven[j], P) for j in range(TILES)]
-        v_mx = [quantize(f"v{b}", v_woven[b], DV) for b in range(B)]
-        mixed = [mix(j, w_mx[j], v_mx[j // HALVES]) for j in range(TILES)]
+        w_woven = [sb(f"w_woven{b}", [P, NQ, PACK], BF16) for b in range(B)]
+        for j in range(TILES):
+            weigh(j, soft[j], vs_cols)
+        w_mx = [quantize(f"w{b}", w_woven[b], NQ) for b in range(B)]
+        v_mx = [
+            [quantize("v0", first_woven, DV)],
+            [quantize(f"v1{h}", second_woven[h], P) for h in range(PLANES)],
+        ]
+        mixed = [mix(j, w_mx[j // HALVES], v_mx[j // HALVES]) for j in range(TILES)]
         for j in range(TILES):
             finish(j, mixed[j])

@@ -47,7 +47,6 @@ def tile_attend_soft_sink_gate_segb2q256n512t2048_kernel(
         v_pool = sb("v_pool", [P, 2 * T], BF16)
         neg_logits = sb("neg_logits", [P, TILES, ROW], F32)
         q_planes = sb("q_planes", [P, B * PASSES * NQ], U8)
-        q_codes = sb("q_codes", [P, B * PASSES, NQ], I32)
         ks_got = sb("ks_got", [P, B * N], U8)
         sink_rows = sb("sink_rows", [P, P], F32)
         gate = sb("gate", [P, TILES * DV], F32)
@@ -88,6 +87,7 @@ def tile_attend_soft_sink_gate_segb2q256n512t2048_kernel(
         load_values(0, 1)
         load_keys(1)
         load_values(1, 0)
+        q_codes = sb("q_codes", [P, B * PASSES, NQ], I32, tag="v_raw00")
         nc.sync.dma_start(out=q_codes[:], in_=q_words.rearrange("b o p q r -> p (b o) (q r)").bitcast(I32))
 
         def listed(b):
@@ -100,8 +100,8 @@ def tile_attend_soft_sink_gate_segb2q256n512t2048_kernel(
                 out=k_planes[32 * quad : 32 * quad + 4, :].bitcast(I32).rearrange("f (o n) -> f o n", o=PASSES),
                 in_=ks_got[KS_ROW0 + 8 * quad : KS_ROW0 + 8 * quad + 8, :].bitcast(I32),
             )
-        load_values(1, 1)
-        og_sb = sb("og_sb", [P, TILES, DV], F32)
+        load_values(1, 1, tag="v_raw01")
+        og_sb = sb("og_sb", [P, TILES, DV], F32, tag="ks_got")
         nc.sync.dma_start(out=og_sb[:], in_=og.rearrange("b (h p) e -> p (b h) e", p=P))
 
         def cast_values(b, h):
@@ -118,14 +118,14 @@ def tile_attend_soft_sink_gate_segb2q256n512t2048_kernel(
             )
             return v_got
 
-        def turn_values(name, got, bank):
+        def turn_values(name, got, bank, tag=""):
             count = len(got)
             turned = psum.tile([P, count, 2, P], F32, name="v_turned", tag=f"bank{bank}")
             for h in range(count):
                 words = got[h][:].rearrange("p u s e -> p (u s e)").bitcast(F32)
                 for u in range(2):
                     nc.tensor.transpose(turned[:, h, u, :], words[:, u * P : (u + 1) * P], ident[:])
-            v_woven = sb(name, [P, count * P, PACK], BF16)
+            v_woven = sb(name, [P, count * P, PACK], BF16, tag=tag)
             nc.scalar.copy(
                 out=v_woven[:].rearrange("p e t -> p (e t)").bitcast(F32).rearrange("p (h e u) -> p h e u", h=count, u=2),
                 in_=turned[:].rearrange("p h u e -> p h e u"),
@@ -256,9 +256,9 @@ def tile_attend_soft_sink_gate_segb2q256n512t2048_kernel(
         accs = [scores(b, h, k_codes[b]) for b in range(B) for h in range(HALVES)]
         cast_values(1, 0)
         v_got[1, 0] = gather_values(1, 0)
+        first_woven = turn_values("v_woven0", [v_got[0, h] for h in range(PLANES)], 6, tag="v_raw10")
         cast_values(1, 1)
         soft = [softmax(j, accs[j]) for j in range(TILES)]
-        first_woven = turn_values("v_woven0", [v_got[0, h] for h in range(PLANES)], 0)
         second_woven = [turn_values("v_woven10", [v_got[1, 0]], 1)]
         v_got[1, 1] = gather_values(1, 1)
         make_gate(range(TILES - 1), tag="neg_logits")

@@ -44,102 +44,46 @@ def tile_attend_soft_sink_gate_segb2q256n512t2048_kernel(
         k_pool = sb("k_pool", [P, T], I32)
         ks_pool = sb("ks_pool", [P, T], U8)
         vs_pool = sb("vs_pool", [P, T], F32)
-        v_pool = sb("v_pool", [P, 2 * T], BF16)
         neg_logits = sb("neg_logits", [P, TILES, ROW], F32)
         q_planes = sb("q_planes", [P, B * PASSES * NQ], U8)
         ks_got = sb("ks_got", [P, B * N], U8)
+        vs_got = sb("vs_got", [P, B * N], F32)
         sink_rows = sb("sink_rows", [P, P], F32)
         gate = sb("gate", [P, TILES * DV], F32)
         ident = sb("ident", [P, P], F32)
         totals = sb("totals", [P, TILES], F32)
         inverses = sb("inverses", [P, TILES], F32)
+        k_planes = sb("k_planes", [P, PASSES * B * N], U8)
 
-        nc.vector.memset(sink_rows[:], 0.0)
+        nc.gpsimd.memset(ident[:], 0.0)
         nc.vector.memset(vs_pool[:, 0:SEG].bitcast(I32), 0)
         nc.gpsimd.memset(vs_pool[:, SEG:T].bitcast(I32), 0)
         nc.vector.memset(ks_pool[0:KS_ROW0, :].bitcast(I32), 0)
-        make_identity(nc, ident[:])
+        nc.scalar.activation(out=sink_rows[:], in_=ident[:], func=ACT.Copy)
+        make_identity(nc, ident[:], nomemset=True)
 
         k_flat = k_words[0].rearrange("p t r -> p (t r)").bitcast(I32)
-
-        nc.sync.dma_start(offsets[:], offs)
-        nc.sync.dma_start(
-            out=ks_pool[KS_ROW0:P, :].bitcast(I32), in_=k_scales.rearrange("o f t -> f o t").bitcast(I32)
-        )
-        v_raw = {}
+        v_pool, q_codes = {}, {}
 
         def load_values(b, h, tag=""):
-            v_raw[b, h] = sb(f"v_raw{b}{h}", [P, SEG], F32, tag=tag)
-            nc.sync.dma_start(out=v_raw[b, h][:], in_=vT[h * P : (h + 1) * P, b * SEG : (b + 1) * SEG])
+            v_pool[b, h] = sb(f"v_pool{b}{h}", [P, (b + 1) * SEG], F32, tag=tag)
+            nc.sync.dma_start(
+                out=v_pool[b, h][:, b * SEG : (b + 1) * SEG], in_=vT[h * P : (h + 1) * P, b * SEG : (b + 1) * SEG]
+            )
 
         def load_keys(b):
             nc.sync.dma_start(out=k_pool[:, b * SEG : (b + 1) * SEG], in_=k_flat[:, b * SEG : (b + 1) * SEG])
 
-        for quad in range(4):
-            nc.scalar.dma_start(
-                out=q_planes[32 * quad : 32 * quad + 4, :].bitcast(I32).rearrange("f (g q) -> f g q", g=B * PASSES),
-                in_=q_scales[:, :, 4 * quad : 4 * quad + 4, :].rearrange("b o f q -> f (b o) q").bitcast(I32),
-            )
-        load_values(0, 0)
-        load_keys(0)
-        nc.sync.dma_start(out=vs_pool[0:1, :], in_=vs[0:1, :])
-        nc.sync.dma_start(out=sink_rows[0:TILES, :], in_=sink.rearrange("b (h p) one -> (b h) (p one)", p=P))
-        load_values(0, 1)
-        load_keys(1)
-        load_values(1, 0)
-        q_codes = sb("q_codes", [P, B * PASSES, NQ], I32, tag="v_raw00")
-        nc.sync.dma_start(out=q_codes[:], in_=q_words.rearrange("b o p q r -> p (b o) (q r)").bitcast(I32))
+        def load_queries(b, tag=""):
+            q_codes[b] = sb(f"q_codes{b}", [P, PASSES, NQ], I32, tag=tag)
+            nc.sync.dma_start(out=q_codes[b][:], in_=q_words[b].rearrange("o p q r -> p o (q r)").bitcast(I32))
 
         def listed(b):
             return offsets[:, b * LIST_COLS : (b + 1) * LIST_COLS]
 
-        nc.vector.tensor_copy(ks_got[:], ks_pool[:].indirect(offsets[:]))
-        k_planes = sb("k_planes", [P, PASSES * B * N], U8)
-        for quad in range(4):
-            nc.sync.dma_start(
-                out=k_planes[32 * quad : 32 * quad + 4, :].bitcast(I32).rearrange("f (o n) -> f o n", o=PASSES),
-                in_=ks_got[KS_ROW0 + 8 * quad : KS_ROW0 + 8 * quad + 8, :].bitcast(I32),
-            )
-        load_values(1, 1, tag="v_raw01")
-        og_sb = sb("og_sb", [P, TILES, DV], F32, tag="ks_got")
-        nc.sync.dma_start(out=og_sb[:], in_=og.rearrange("b (h p) e -> p (b h) e", p=P))
-
-        def cast_values(b, h):
-            plane = b * PLANES + h
-            nc.scalar.activation(out=v_pool[:, plane * SEG : (plane + 1) * SEG], in_=v_raw[b, h][:], func=ACT.Copy)
-
-        def gather_values(b, h):
-            plane = b * PLANES + h
-            v_got = sb(f"v_got{b}{h}", [P, 2, P, 2], BF16)
-            nc.scalar.activation(
-                out=v_got[:].rearrange("p u s e -> p s u e"),
-                in_=v_pool[:, (plane - b) * SEG : (plane + 1) * SEG].indirect(listed(b)),
-                func=ACT.Copy,
-            )
-            return v_got
-
-        def turn_values(name, got, bank, tag=""):
-            count = len(got)
-            turned = psum.tile([P, count, 2, P], F32, name="v_turned", tag=f"bank{bank}")
-            for h in range(count):
-                words = got[h][:].rearrange("p u s e -> p (u s e)").bitcast(F32)
-                for u in range(2):
-                    nc.tensor.transpose(turned[:, h, u, :], words[:, u * P : (u + 1) * P], ident[:])
-            v_woven = sb(name, [P, count * P, PACK], BF16, tag=tag)
-            nc.scalar.copy(
-                out=v_woven[:].rearrange("p e t -> p (e t)").bitcast(F32).rearrange("p (h e u) -> p h e u", h=count, u=2),
-                in_=turned[:].rearrange("p h u e -> p h e u"),
-            )
-            return v_woven
-
-        vs_cols = sb("vs_cols", [P, B, 8], F32)
-
         def gather_keys(b):
             k_got = sb(f"k_got{b}", [P, N], U32)
             nc.vector.tensor_copy(k_got[:], k_pool[:, 0 : (b + 1) * SEG].bitcast(U32).indirect(listed(b)))
-            vs_got = sb(f"vs_got{b}", [P, N], F32)
-            nc.vector.tensor_copy(vs_got[:], vs_pool[:, 0 : (b + 1) * SEG].indirect(listed(b)))
-            nc.sync.dma_start(out=vs_cols[:, b, 0:PACK], in_=vs_got[0:1, :])
             k_codes = sb(f"k_codes{b}", [P, PASSES, 2 * N], U8)
             nc.vector.tensor_copy(
                 out=k_codes[:].bitcast(U16),
@@ -147,13 +91,59 @@ def tile_attend_soft_sink_gate_segb2q256n512t2048_kernel(
             )
             return k_codes
 
+        nc.sync.dma_start(offsets[:], offs)
+        nc.sync.dma_start(
+            out=ks_pool[KS_ROW0:P, :].bitcast(I32), in_=k_scales.rearrange("o f t -> f o t").bitcast(I32)
+        )
+        for quad in range(4):
+            nc.sync.dma_start(
+                out=q_planes[32 * quad : 32 * quad + 4, :].bitcast(I32).rearrange("f (g q) -> f g q", g=B * PASSES),
+                in_=q_scales[:, :, 4 * quad : 4 * quad + 4, :].rearrange("b o f q -> f (b o) q").bitcast(I32),
+            )
+        load_values(0, 0)
+        load_keys(0)
+        nc.sync.dma_start(out=vs_pool[0:1, :], in_=vs[0:1, :])
+        load_keys(1)
+        load_queries(0)
+        nc.sync.dma_start(out=sink_rows[0:TILES, :], in_=sink.rearrange("b (h p) one -> (b h) (p one)", p=P))
+
+        nc.vector.tensor_copy(ks_got[:], ks_pool[:].indirect(offsets[:]))
+        for quad in range(4):
+            nc.sync.dma_start(
+                out=k_planes[32 * quad : 32 * quad + 4, :].bitcast(I32).rearrange("f (o n) -> f o n", o=PASSES),
+                in_=ks_got[KS_ROW0 + 8 * quad : KS_ROW0 + 8 * quad + 8, :].bitcast(I32),
+            )
+        k_codes = [gather_keys(b) for b in range(B)]
+        load_values(0, 1, tag="ks_pool")
+        load_queries(1, tag="v_pool00")
+        load_values(1, 0, tag="k_got0")
+        load_values(1, 1, tag="k_pool")
+        vs_cols = sb("vs_cols", [P, B, 8], F32, tag="k_got1")
+        og_sb = sb("og_sb", [P, TILES, DV], F32, tag="k_codes1")
+        nc.sync.dma_start(out=og_sb[:], in_=og.rearrange("b (h p) e -> p (b h) e", p=P))
+
+        def gather_values(b, h, tag=""):
+            v_got = sb(f"v_got{b}{h}", [P, N], BF16, tag=tag)
+            nc.scalar.activation(out=v_got[:], in_=v_pool[b, h][:].indirect(listed(b)), func=ACT.Copy)
+            return v_got
+
+        def turn_values(got, bank, woven):
+            turned = psum.tile([P, 2, P], F32, name="v_turned", tag=f"bank{bank}")
+            words = got[:].bitcast(F32)
+            for u in range(2):
+                nc.tensor.transpose(turned[:, u, :], words[:, u : N // 2 : 2], ident[:])
+            nc.scalar.copy(
+                out=woven.rearrange("p e t -> p (e t)").bitcast(F32).rearrange("p (e u) -> p e u", u=2),
+                in_=turned[:].rearrange("p u e -> p e u"),
+            )
+
         def scores(b, h, k_codes):
             acc = psum.tile([P, N], F32, name="score", tag=f"bank{b * HALVES + h}")
             for o in range(PASSES):
                 first = (b * PASSES + o) * NQ + h * P
                 nc.tensor.matmul_mx(
                     out=acc[:],
-                    lhsT=q_codes[:, b * PASSES + o, h * P : (h + 1) * P].bitcast(FP8X4),
+                    lhsT=q_codes[b][:, o, h * P : (h + 1) * P].bitcast(FP8X4),
                     lhsT_scale=q_planes[:, first : first + P],
                     rhs=k_codes[:, o, :].bitcast(FP4X4),
                     rhs_scale=k_planes[:, (o * B + b) * N : (o * B + b + 1) * N],
@@ -195,18 +185,18 @@ def tile_attend_soft_sink_gate_segb2q256n512t2048_kernel(
             )
             return codes, plane
 
-        def weigh(j, turned, vs_cols):
+        def weigh(j, turned):
             b, h = divmod(j, HALVES)
             nc.vector.tensor_tensor(
                 out=w_woven[b][:, h * P : (h + 1) * P, :],
                 in0=turned[:].rearrange("p t q -> p q t"),
-                in1=vs_cols[:, j // HALVES, 0:PACK].unsqueeze(1).to_broadcast([P, P, PACK]),
+                in1=vs_cols[:, b, 0:PACK].unsqueeze(1).to_broadcast([P, P, PACK]),
                 op=ALU.mult,
             )
 
         def mix(j, w_mx, v_parts):
             rows = slice(j % HALVES * P, (j % HALVES + 1) * P)
-            acc = psum.tile([P, DV], F32, name="mixed", tag=f"bank{(j + 2) % TILES}")
+            acc = psum.tile([P, DV], F32, name="mixed", tag=f"bank{2 + j}")
             width = DV // len(v_parts)
             for c, v_mx in enumerate(v_parts):
                 nc.tensor.matmul_mx(
@@ -221,7 +211,7 @@ def tile_attend_soft_sink_gate_segb2q256n512t2048_kernel(
             return acc
 
         def finish(j, acc):
-            result = sb(f"result{j}", [P, DV], F32, tag="v_woven11" if j == 0 else "")
+            result = sb(f"result{j}", [P, DV], F32)
             nc.vector.scalar_tensor_tensor(
                 out=result[:],
                 in0=acc[:],
@@ -246,28 +236,31 @@ def tile_attend_soft_sink_gate_segb2q256n512t2048_kernel(
                     nc.scalar.activation(out=gate[:, cols], in_=half_tanh[:, c, :], func=ACT.Copy, scale=0.5, bias=0.5)
 
         v_got = {}
-        for h in range(PLANES):
-            cast_values(0, h)
-            v_got[0, h] = gather_values(0, h)
-        sink_turned = psum.tile([P, P], F32, name="sink_turned", tag="bank4")
+        v_got[0, 0] = gather_values(0, 0)
+        nc.scalar.activation(out=vs_got[:], in_=vs_pool[:].indirect(offsets[:]), func=ACT.Copy)
+        for b in range(B):
+            nc.sync.dma_start(out=vs_cols[:, b, 0:PACK], in_=vs_got[0:1, b * N : (b + 1) * N])
+        first_woven = sb("v_woven0", [P, DV, PACK], BF16)
+        turn_values(v_got[0, 0], 7, first_woven[:, 0:P, :])
+        sink_turned = psum.tile([P, P], F32, name="sink_turned", tag="bank6")
         nc.tensor.transpose(sink_turned[:], sink_rows[:], ident[:])
         nc.scalar.activation(out=neg_logits[:, :, N], in_=sink_turned[:, 0:TILES], func=ACT.Copy, scale=-1.0)
-        k_codes = [gather_keys(b) for b in range(B)]
+        v_got[0, 1] = gather_values(0, 1)
         accs = [scores(b, h, k_codes[b]) for b in range(B) for h in range(HALVES)]
-        cast_values(1, 0)
-        v_got[1, 0] = gather_values(1, 0)
-        first_woven = turn_values("v_woven0", [v_got[0, h] for h in range(PLANES)], 6, tag="v_raw10")
-        cast_values(1, 1)
-        soft = [softmax(j, accs[j]) for j in range(TILES)]
-        second_woven = [turn_values("v_woven10", [v_got[1, 0]], 1)]
-        v_got[1, 1] = gather_values(1, 1)
-        make_gate(range(TILES - 1), tag="neg_logits")
-        second_woven.append(turn_values("v_woven11", [v_got[1, 1]], 4))
-        make_gate(range(TILES - 1, TILES), tag="v_got11")
+        soft = [softmax(0, accs[0])]
+        turn_values(v_got[0, 1], 0, first_woven[:, P:DV, :])
+        soft.extend(softmax(j, accs[j]) for j in range(1, TILES))
+        second_woven = [sb(f"v_woven1{h}", [P, P, PACK], BF16) for h in range(PLANES)]
+        v_got[1, 0] = gather_values(1, 0, tag=f"neg_max{TILES - 1}")
+        v_got[1, 1] = gather_values(1, 1, tag="neg_logits")
+        turn_values(v_got[1, 0], 1, second_woven[0][:])
+        make_gate(range(1), tag="k_pool")
+        turn_values(v_got[1, 1], 0, second_woven[1][:])
+        make_gate(range(1, TILES), tag="neg_logits")
         nc.vector.reciprocal(inverses[:], totals[:])
         w_woven = [sb(f"w_woven{b}", [P, NQ, PACK], BF16) for b in range(B)]
         for j in range(TILES):
-            weigh(j, soft[j], vs_cols)
+            weigh(j, soft[j])
         w_mx = [quantize(f"w{b}", w_woven[b], NQ) for b in range(B)]
         v_mx = [
             [quantize("v0", first_woven, DV)],

@@ -95,15 +95,16 @@ def tile_attend_soft_sink_gate_segb2q256n512t2048_kernel(
         nc.sync.dma_start(
             out=ks_pool[KS_ROW0:P, :].bitcast(I32), in_=k_scales.rearrange("o f t -> f o t").bitcast(I32)
         )
+        load_values(0, 0)
+        load_keys(0)
+        nc.sync.dma_start(out=vs_pool[0:1, :], in_=vs[0:1, :])
         for quad in range(4):
             nc.sync.dma_start(
                 out=q_planes[32 * quad : 32 * quad + 4, :].bitcast(I32).rearrange("f (g q) -> f g q", g=B * PASSES),
                 in_=q_scales[:, :, 4 * quad : 4 * quad + 4, :].rearrange("b o f q -> f (b o) q").bitcast(I32),
             )
-        load_values(0, 0)
-        load_keys(0)
-        nc.sync.dma_start(out=vs_pool[0:1, :], in_=vs[0:1, :])
         load_keys(1)
+        load_values(0, 1)
         load_queries(0)
         nc.sync.dma_start(out=sink_rows[0:TILES, :], in_=sink.rearrange("b (h p) one -> (b h) (p one)", p=P))
 
@@ -114,12 +115,11 @@ def tile_attend_soft_sink_gate_segb2q256n512t2048_kernel(
                 in_=ks_got[KS_ROW0 + 8 * quad : KS_ROW0 + 8 * quad + 8, :].bitcast(I32),
             )
         k_codes = [gather_keys(b) for b in range(B)]
-        load_values(0, 1, tag="ks_pool")
-        load_queries(1, tag="v_pool00")
-        load_values(1, 0, tag="k_got0")
+        load_values(1, 0, tag="ks_pool")
+        load_queries(1, tag="k_got0")
         load_values(1, 1, tag="k_pool")
         vs_cols = sb("vs_cols", [P, B, 8], F32, tag="k_got1")
-        og_sb = sb("og_sb", [P, TILES, DV], F32, tag="k_codes1")
+        og_sb = sb("og_sb", [P, TILES, DV], F32, tag="k_codes0")
         nc.sync.dma_start(out=og_sb[:], in_=og.rearrange("b (h p) e -> p (b h) e", p=P))
 
         def gather_values(b, h, tag=""):
@@ -196,15 +196,15 @@ def tile_attend_soft_sink_gate_segb2q256n512t2048_kernel(
 
         def mix(j, w_mx, v_parts):
             rows = slice(j % HALVES * P, (j % HALVES + 1) * P)
-            acc = psum.tile([P, DV], F32, name="mixed", tag=f"bank{2 + j}")
+            acc = psum.tile([P, DV], F32, name="mixed", tag=f"bank{4 + j}")
             width = DV // len(v_parts)
             for c, v_mx in enumerate(v_parts):
                 nc.tensor.matmul_mx(
                     out=acc[:, c * width : (c + 1) * width],
                     lhsT=w_mx[0][:, rows].bitcast(FP8X4),
                     lhsT_scale=w_mx[1][:, rows],
-                    rhs=v_mx[0][:].bitcast(FP8X4),
-                    rhs_scale=v_mx[1][:],
+                    rhs=v_mx[0].bitcast(FP8X4),
+                    rhs_scale=v_mx[1],
                     start=True,
                     stop=True,
                 )
@@ -240,31 +240,34 @@ def tile_attend_soft_sink_gate_segb2q256n512t2048_kernel(
         nc.scalar.activation(out=vs_got[:], in_=vs_pool[:].indirect(offsets[:]), func=ACT.Copy)
         for b in range(B):
             nc.sync.dma_start(out=vs_cols[:, b, 0:PACK], in_=vs_got[0:1, b * N : (b + 1) * N])
-        first_woven = sb("v_woven0", [P, DV, PACK], BF16)
-        turn_values(v_got[0, 0], 7, first_woven[:, 0:P, :])
+        first_woven = sb("first_woven", [P, P, PACK], BF16)
+        turn_values(v_got[0, 0], 7, first_woven[:])
+        v_got[0, 1] = gather_values(0, 1)
         sink_turned = psum.tile([P, P], F32, name="sink_turned", tag="bank6")
         nc.tensor.transpose(sink_turned[:], sink_rows[:], ident[:])
         nc.scalar.activation(out=neg_logits[:, :, N], in_=sink_turned[:, 0:TILES], func=ACT.Copy, scale=-1.0)
-        v_got[0, 1] = gather_values(0, 1)
+        v_got[1, 0] = gather_values(1, 0)
         accs = [scores(b, h, k_codes[b]) for b in range(B) for h in range(HALVES)]
-        soft = [softmax(0, accs[0])]
-        turn_values(v_got[0, 1], 0, first_woven[:, P:DV, :])
-        soft.extend(softmax(j, accs[j]) for j in range(1, TILES))
-        second_woven = [sb(f"v_woven1{h}", [P, P, PACK], BF16) for h in range(PLANES)]
-        v_got[1, 0] = gather_values(1, 0, tag=f"neg_max{TILES - 1}")
+        soft = [softmax(j, accs[j]) for j in range(TILES)]
         v_got[1, 1] = gather_values(1, 1, tag="neg_logits")
-        turn_values(v_got[1, 0], 1, second_woven[0][:])
-        make_gate(range(1), tag="k_pool")
-        turn_values(v_got[1, 1], 0, second_woven[1][:])
-        make_gate(range(1, TILES), tag="neg_logits")
+        make_gate(range(HALVES), tag="k_pool")
+        middle_woven = sb("middle_woven", [P, 2 * P, PACK], BF16, tag=f"neg_max{TILES - 1}")
+        turn_values(v_got[0, 1], 2, middle_woven[:, 0:P, :])
+        turn_values(v_got[1, 0], 3, middle_woven[:, P : 2 * P, :])
+        last_woven = sb("last_woven", [P, P, PACK], BF16)
+        turn_values(v_got[1, 1], 0, last_woven[:])
+        make_gate(range(HALVES, TILES), tag="neg_logits")
         nc.vector.reciprocal(inverses[:], totals[:])
         w_woven = [sb(f"w_woven{b}", [P, NQ, PACK], BF16) for b in range(B)]
         for j in range(TILES):
             weigh(j, soft[j])
         w_mx = [quantize(f"w{b}", w_woven[b], NQ) for b in range(B)]
+        first = quantize("v_first", first_woven, P)
+        middle = quantize("v_middle", middle_woven, 2 * P)
+        last = quantize("v_last", last_woven, P)
         v_mx = [
-            [quantize("v0", first_woven, DV)],
-            [quantize(f"v1{h}", second_woven[h], P) for h in range(PLANES)],
+            [(first[0][:], first[1][:]), (middle[0][:, 0:P], middle[1][:, 0:P])],
+            [(middle[0][:, P : 2 * P], middle[1][:, P : 2 * P]), (last[0][:], last[1][:])],
         ]
         mixed = [mix(j, w_mx[j // HALVES], v_mx[j // HALVES]) for j in range(TILES)]
         for j in range(TILES):

@@ -104,7 +104,6 @@ def tile_attend_soft_sink_gate_segb2q256n512t2048_kernel(
                 in_=q_scales[:, :, 4 * quad : 4 * quad + 4, :].rearrange("b o f q -> f (b o) q").bitcast(I32),
             )
         load_keys(1)
-        load_values(0, 1)
         load_queries(0)
         nc.sync.dma_start(out=sink_rows[0:TILES, :], in_=sink.rearrange("b (h p) one -> (b h) (p one)", p=P))
 
@@ -115,8 +114,9 @@ def tile_attend_soft_sink_gate_segb2q256n512t2048_kernel(
                 in_=ks_got[KS_ROW0 + 8 * quad : KS_ROW0 + 8 * quad + 8, :].bitcast(I32),
             )
         k_codes = [gather_keys(b) for b in range(B)]
-        load_values(1, 0, tag="ks_pool")
+        load_values(0, 1, tag="ks_pool")
         load_queries(1, tag="k_got0")
+        load_values(1, 0, tag="vs_pool")
         load_values(1, 1, tag="k_pool")
         vs_cols = sb("vs_cols", [P, B, 8], F32, tag="k_got1")
         og_sb = sb("og_sb", [P, TILES, DV], F32, tag="k_codes0")
@@ -127,12 +127,12 @@ def tile_attend_soft_sink_gate_segb2q256n512t2048_kernel(
             nc.scalar.activation(out=v_got[:], in_=v_pool[b, h][:].indirect(listed(b)), func=ACT.Copy)
             return v_got
 
-        def turn_values(got, bank, woven):
+        def turn_values(got, bank, woven, copy):
             turned = psum.tile([P, 2, P], F32, name="v_turned", tag=f"bank{bank}")
             words = got[:].bitcast(F32)
             for u in range(2):
                 nc.tensor.transpose(turned[:, u, :], words[:, u : N // 2 : 2], ident[:])
-            nc.scalar.copy(
+            copy(
                 out=woven.rearrange("p e t -> p (e t)").bitcast(F32).rearrange("p (e u) -> p e u", u=2),
                 in_=turned[:].rearrange("p u e -> p e u"),
             )
@@ -203,8 +203,8 @@ def tile_attend_soft_sink_gate_segb2q256n512t2048_kernel(
                     out=acc[:, c * width : (c + 1) * width],
                     lhsT=w_mx[0][:, rows].bitcast(FP8X4),
                     lhsT_scale=w_mx[1][:, rows],
-                    rhs=v_mx[0].bitcast(FP8X4),
-                    rhs_scale=v_mx[1],
+                    rhs=v_mx[0][:].bitcast(FP8X4),
+                    rhs_scale=v_mx[1][:],
                     start=True,
                     stop=True,
                 )
@@ -240,34 +240,32 @@ def tile_attend_soft_sink_gate_segb2q256n512t2048_kernel(
         nc.scalar.activation(out=vs_got[:], in_=vs_pool[:].indirect(offsets[:]), func=ACT.Copy)
         for b in range(B):
             nc.sync.dma_start(out=vs_cols[:, b, 0:PACK], in_=vs_got[0:1, b * N : (b + 1) * N])
-        first_woven = sb("first_woven", [P, P, PACK], BF16)
-        turn_values(v_got[0, 0], 7, first_woven[:])
-        v_got[0, 1] = gather_values(0, 1)
+        first_woven = sb("first_woven", [P, DV, PACK], BF16)
+        turn_values(v_got[0, 0], 7, first_woven[:, 0:P, :], nc.scalar.copy)
         sink_turned = psum.tile([P, P], F32, name="sink_turned", tag="bank6")
         nc.tensor.transpose(sink_turned[:], sink_rows[:], ident[:])
         nc.scalar.activation(out=neg_logits[:, :, N], in_=sink_turned[:, 0:TILES], func=ACT.Copy, scale=-1.0)
-        v_got[1, 0] = gather_values(1, 0)
+        v_got[0, 1] = gather_values(0, 1)
         accs = [scores(b, h, k_codes[b]) for b in range(B) for h in range(HALVES)]
         soft = [softmax(j, accs[j]) for j in range(TILES)]
+        v_got[1, 0] = gather_values(1, 0, tag=f"neg_max{TILES - 1}")
         v_got[1, 1] = gather_values(1, 1, tag="neg_logits")
-        make_gate(range(HALVES), tag="k_pool")
-        middle_woven = sb("middle_woven", [P, 2 * P, PACK], BF16, tag=f"neg_max{TILES - 1}")
-        turn_values(v_got[0, 1], 2, middle_woven[:, 0:P, :])
-        turn_values(v_got[1, 0], 3, middle_woven[:, P : 2 * P, :])
         last_woven = sb("last_woven", [P, P, PACK], BF16)
-        turn_values(v_got[1, 1], 0, last_woven[:])
+        make_gate(range(HALVES), tag="k_pool")
+        turn_values(v_got[1, 1], 0, last_woven[:], nc.scalar.copy)
         make_gate(range(HALVES, TILES), tag="neg_logits")
         nc.vector.reciprocal(inverses[:], totals[:])
         w_woven = [sb(f"w_woven{b}", [P, NQ, PACK], BF16) for b in range(B)]
         for j in range(TILES):
             weigh(j, soft[j])
+        turn_values(v_got[0, 1], 2, first_woven[:, P:DV, :], nc.vector.tensor_copy)
         w_mx = [quantize(f"w{b}", w_woven[b], NQ) for b in range(B)]
-        first = quantize("v_first", first_woven, P)
-        middle = quantize("v_middle", middle_woven, 2 * P)
-        last = quantize("v_last", last_woven, P)
+        third_woven = sb("third_woven", [P, P, PACK], BF16, tag="w_woven0")
+        turn_values(v_got[1, 0], 3, third_woven[:], nc.vector.tensor_copy)
+        second_woven = [third_woven, last_woven]
         v_mx = [
-            [(first[0][:], first[1][:]), (middle[0][:, 0:P], middle[1][:, 0:P])],
-            [(middle[0][:, P : 2 * P], middle[1][:, P : 2 * P]), (last[0][:], last[1][:])],
+            [quantize("v0", first_woven, DV)],
+            [quantize(f"v1{h}", second_woven[h], P) for h in range(PLANES)],
         ]
         mixed = [mix(j, w_mx[j // HALVES], v_mx[j // HALVES]) for j in range(TILES)]
         for j in range(TILES):

@@ -27,6 +27,8 @@ LIST_COLS = N // 16
 ROW = N + 8
 KS_ROW0 = 96
 PLANES = DV // P
+QUADS = (0, 2, 1, 3)
+VS_ROW = 16
 
 
 def tile_attend_soft_sink_gate_segb2q256n512t2048_kernel(
@@ -97,8 +99,8 @@ def tile_attend_soft_sink_gate_segb2q256n512t2048_kernel(
         )
         load_values(0, 0)
         load_keys(0)
-        nc.sync.dma_start(out=vs_pool[0:1, :], in_=vs[0:1, :])
-        for quad in range(4):
+        nc.sync.dma_start(out=vs_pool[VS_ROW : VS_ROW + 1, :], in_=vs[0:1, :])
+        for quad in QUADS:
             nc.sync.dma_start(
                 out=q_planes[32 * quad : 32 * quad + 4, :].bitcast(I32).rearrange("f (g q) -> f g q", g=B * PASSES),
                 in_=q_scales[:, :, 4 * quad : 4 * quad + 4, :].rearrange("b o f q -> f (b o) q").bitcast(I32),
@@ -108,7 +110,7 @@ def tile_attend_soft_sink_gate_segb2q256n512t2048_kernel(
         nc.sync.dma_start(out=sink_rows[0:TILES, :], in_=sink.rearrange("b (h p) one -> (b h) (p one)", p=P))
 
         nc.vector.tensor_copy(ks_got[:], ks_pool[:].indirect(offsets[:]))
-        for quad in range(4):
+        for quad in QUADS:
             nc.sync.dma_start(
                 out=k_planes[32 * quad : 32 * quad + 4, :].bitcast(I32).rearrange("f (o n) -> f o n", o=PASSES),
                 in_=ks_got[KS_ROW0 + 8 * quad : KS_ROW0 + 8 * quad + 8, :].bitcast(I32),
@@ -239,7 +241,7 @@ def tile_attend_soft_sink_gate_segb2q256n512t2048_kernel(
         v_got[0, 0] = gather_values(0, 0)
         nc.scalar.activation(out=vs_got[:], in_=vs_pool[:].indirect(offsets[:]), func=ACT.Copy)
         for b in range(B):
-            nc.sync.dma_start(out=vs_cols[:, b, 0:PACK], in_=vs_got[0:1, b * N : (b + 1) * N])
+            nc.sync.dma_start(out=vs_cols[:, b, 0:PACK], in_=vs_got[VS_ROW : VS_ROW + 1, b * N : (b + 1) * N])
         first_woven = sb("first_woven", [P, DV, PACK], BF16)
         turn_values(v_got[0, 0], 7, first_woven[:, 0:P, :], nc.scalar.copy)
         sink_turned = psum.tile([P, P], F32, name="sink_turned", tag="bank6")

@@ -29,6 +29,7 @@ KS_ROW0 = 96
 PLANES = DV // P
 QUADS = (0, 2, 1, 3)
 VS_ROW = 16
+SINK_ROW = 24
 
 
 def tile_attend_soft_sink_gate_segb2q256n512t2048_kernel(
@@ -43,19 +44,15 @@ def tile_attend_soft_sink_gate_segb2q256n512t2048_kernel(
             return keep.tile(shape, dtype, name=name, tag=tag or name, align_bytes=64)
 
         offsets = keep.tile([P, B * LIST_COLS], U16, name="offsets")
-        k_pool = sb("k_pool", [P, T], I32)
         ks_pool = sb("ks_pool", [P, T], U8)
         vs_pool = sb("vs_pool", [P, T], F32)
         neg_logits = sb("neg_logits", [P, TILES, ROW], F32)
         q_planes = sb("q_planes", [P, B * PASSES * NQ], U8)
-        ks_got = sb("ks_got", [P, B * N], U8)
-        vs_got = sb("vs_got", [P, B * N], F32)
         sink_rows = sb("sink_rows", [P, P], F32)
         gate = sb("gate", [P, TILES * DV], F32)
         ident = sb("ident", [P, P], F32)
         totals = sb("totals", [P, TILES], F32)
         inverses = sb("inverses", [P, TILES], F32)
-        k_planes = sb("k_planes", [P, PASSES * B * N], U8)
 
         nc.gpsimd.memset(ident[:], 0.0)
         nc.vector.memset(vs_pool[:, 0:SEG].bitcast(I32), 0)
@@ -65,7 +62,7 @@ def tile_attend_soft_sink_gate_segb2q256n512t2048_kernel(
         make_identity(nc, ident[:], nomemset=True)
 
         k_flat = k_words[0].rearrange("p t r -> p (t r)").bitcast(I32)
-        v_pool, q_codes = {}, {}
+        v_pool, q_codes, k_pool, k_got, k_codes, k_planes = {}, {}, {}, {}, {}, {}
 
         def load_values(b, h, tag=""):
             v_pool[b, h] = sb(f"v_pool{b}{h}", [P, (b + 1) * SEG], F32, tag=tag)
@@ -74,7 +71,8 @@ def tile_attend_soft_sink_gate_segb2q256n512t2048_kernel(
             )
 
         def load_keys(b):
-            nc.sync.dma_start(out=k_pool[:, b * SEG : (b + 1) * SEG], in_=k_flat[:, b * SEG : (b + 1) * SEG])
+            k_pool[b] = sb(f"k_pool{b}", [P, (b + 1) * SEG], I32)
+            nc.sync.dma_start(out=k_pool[b][:, b * SEG : (b + 1) * SEG], in_=k_flat[:, b * SEG : (b + 1) * SEG])
 
         def load_queries(b, tag=""):
             q_codes[b] = sb(f"q_codes{b}", [P, PASSES, NQ], I32, tag=tag)
@@ -83,23 +81,47 @@ def tile_attend_soft_sink_gate_segb2q256n512t2048_kernel(
         def listed(b):
             return offsets[:, b * LIST_COLS : (b + 1) * LIST_COLS]
 
+        def gather_key_scales(b):
+            ks_got = sb(f"ks_got{b}", [P, N], U8)
+            nc.vector.tensor_copy(ks_got[:], ks_pool[:].indirect(listed(b)))
+            return ks_got
+
+        def move_key_scales(b, ks_got):
+            k_planes[b] = sb(f"k_planes{b}", [P, PASSES * N], U8)
+            for quad in QUADS:
+                nc.sync.dma_start(
+                    out=k_planes[b][32 * quad : 32 * quad + 4, :].bitcast(I32).rearrange("f (o n) -> f o n", o=PASSES),
+                    in_=ks_got[KS_ROW0 + 8 * quad : KS_ROW0 + 8 * quad + 8, :].bitcast(I32),
+                )
+
         def gather_keys(b):
-            k_got = sb(f"k_got{b}", [P, N], U32)
-            nc.vector.tensor_copy(k_got[:], k_pool[:, 0 : (b + 1) * SEG].bitcast(U32).indirect(listed(b)))
-            k_codes = sb(f"k_codes{b}", [P, PASSES, 2 * N], U8)
+            k_got[b] = sb(f"k_got{b}", [P, N], U32)
+            nc.vector.tensor_copy(k_got[b][:], k_pool[b][:].bitcast(U32).indirect(listed(b)))
+
+        def part_keys(b):
+            k_codes[b] = sb(f"k_codes{b}", [P, PASSES, 2 * N], U8)
             nc.vector.tensor_copy(
-                out=k_codes[:].bitcast(U16),
-                in_=k_got[:].bitcast(U16).rearrange("p (i o) -> p o i", o=PASSES),
+                out=k_codes[b][:].bitcast(U16),
+                in_=k_got[b][:].bitcast(U16).rearrange("p (i o) -> p o i", o=PASSES),
             )
-            return k_codes
+
+        def gather_values(b, h, tag=""):
+            v_got = sb(f"v_got{b}{h}", [P, N], BF16, tag=tag)
+            nc.scalar.activation(out=v_got[:], in_=v_pool[b, h][:].indirect(listed(b)), func=ACT.Copy)
+            return v_got
+
+        def gather_token_scales(b, tag=""):
+            vs_got = sb(f"vs_got{b}", [P, N], F32, tag=tag)
+            nc.scalar.activation(out=vs_got[:], in_=vs_pool[:].indirect(listed(b)), func=ACT.Copy)
+            nc.sync.dma_start(out=vs_cols[:, b, 0:PACK], in_=vs_got[VS_ROW : VS_ROW + 1, :])
 
         nc.sync.dma_start(offsets[:], offs)
         nc.sync.dma_start(
             out=ks_pool[KS_ROW0:P, :].bitcast(I32), in_=k_scales.rearrange("o f t -> f o t").bitcast(I32)
         )
-        load_values(0, 0)
         load_keys(0)
         nc.sync.dma_start(out=vs_pool[VS_ROW : VS_ROW + 1, :], in_=vs[0:1, :])
+        load_values(0, 0)
         for quad in QUADS:
             nc.sync.dma_start(
                 out=q_planes[32 * quad : 32 * quad + 4, :].bitcast(I32).rearrange("f (g q) -> f g q", g=B * PASSES),
@@ -107,27 +129,28 @@ def tile_attend_soft_sink_gate_segb2q256n512t2048_kernel(
             )
         load_keys(1)
         load_queries(0)
-        nc.sync.dma_start(out=sink_rows[0:TILES, :], in_=sink.rearrange("b (h p) one -> (b h) (p one)", p=P))
+        nc.sync.dma_start(
+            out=sink_rows[SINK_ROW : SINK_ROW + TILES, :], in_=sink.rearrange("b (h p) one -> (b h) (p one)", p=P)
+        )
 
-        nc.vector.tensor_copy(ks_got[:], ks_pool[:].indirect(offsets[:]))
-        for quad in QUADS:
-            nc.sync.dma_start(
-                out=k_planes[32 * quad : 32 * quad + 4, :].bitcast(I32).rearrange("f (o n) -> f o n", o=PASSES),
-                in_=ks_got[KS_ROW0 + 8 * quad : KS_ROW0 + 8 * quad + 8, :].bitcast(I32),
-            )
-        k_codes = [gather_keys(b) for b in range(B)]
-        load_values(0, 1, tag="ks_pool")
-        load_queries(1, tag="k_got0")
-        load_values(1, 0, tag="vs_pool")
-        load_values(1, 1, tag="k_pool")
-        vs_cols = sb("vs_cols", [P, B, 8], F32, tag="k_got1")
-        og_sb = sb("og_sb", [P, TILES, DV], F32, tag="k_codes0")
-        nc.sync.dma_start(out=og_sb[:], in_=og.rearrange("b (h p) e -> p (b h) e", p=P))
-
-        def gather_values(b, h, tag=""):
-            v_got = sb(f"v_got{b}{h}", [P, N], BF16, tag=tag)
-            nc.scalar.activation(out=v_got[:], in_=v_pool[b, h][:].indirect(listed(b)), func=ACT.Copy)
-            return v_got
+        move_key_scales(0, gather_key_scales(0))
+        gather_keys(0)
+        load_values(0, 1, tag="k_pool0")
+        second_scales = gather_key_scales(1)
+        load_queries(1, tag="ks_pool")
+        move_key_scales(1, second_scales)
+        part_keys(0)
+        gather_keys(1)
+        part_keys(1)
+        load_values(1, 0, tag="k_got0")
+        vs_cols = sb("vs_cols", [P, B, 8], F32)
+        gather_token_scales(0)
+        v_got = {(0, 0): gather_values(0, 0)}
+        gather_token_scales(1, tag="v_pool00")
+        load_values(1, 1, tag="k_pool1")
+        og_sb = [sb(f"og{b}", [P, HALVES, DV], F32, tag=f"k_codes{b}") for b in range(B)]
+        for b in range(B):
+            nc.sync.dma_start(out=og_sb[b][:], in_=og[b].rearrange("(h p) e -> p h e", p=P))
 
         def turn_values(got, bank, woven, copy):
             turned = psum.tile([P, 2, P], F32, name="v_turned", tag=f"bank{bank}")
@@ -148,7 +171,7 @@ def tile_attend_soft_sink_gate_segb2q256n512t2048_kernel(
                     lhsT=q_codes[b][:, o, h * P : (h + 1) * P].bitcast(FP8X4),
                     lhsT_scale=q_planes[:, first : first + P],
                     rhs=k_codes[:, o, :].bitcast(FP4X4),
-                    rhs_scale=k_planes[:, (o * B + b) * N : (o * B + b + 1) * N],
+                    rhs_scale=k_planes[b][:, o * N : (o + 1) * N],
                     start=(o == 0),
                     stop=(o == PASSES - 1),
                 )
@@ -174,7 +197,7 @@ def tile_attend_soft_sink_gate_segb2q256n512t2048_kernel(
                 scale=-1.0,
                 accum_out=totals[:, j : j + 1],
             )
-            turned = psum.tile([P, PACK, P], F32, name="probs_turned", tag=f"bank{4 + j}")
+            turned = psum.tile([P, PACK, P], F32, name="probs_turned", tag=f"bank{(j + HALVES) % TILES}")
             for t in range(PACK):
                 nc.tensor.transpose(turned[:, t, :], probs[:, t * P : (t + 1) * P], ident[:])
             return turned
@@ -228,7 +251,7 @@ def tile_attend_soft_sink_gate_segb2q256n512t2048_kernel(
         def make_gate(tiles, tag):
             half_tanh = sb(f"half_tanh{tiles[0]}", [P, len(tiles), DV], F32, tag=tag)
             for c, j in enumerate(tiles):
-                nc.scalar.activation(out=half_tanh[:, c, :], in_=og_sb[:, j, :], func=ACT.Tanh, scale=0.5)
+                nc.scalar.activation(out=half_tanh[:, c, :], in_=og_sb[j // HALVES][:, j % HALVES, :], func=ACT.Tanh, scale=0.5)
                 cols = slice(j * DV, (j + 1) * DV)
                 if j < TILES - 1:
                     nc.gpsimd.tensor_scalar(
@@ -237,23 +260,18 @@ def tile_attend_soft_sink_gate_segb2q256n512t2048_kernel(
                 else:
                     nc.scalar.activation(out=gate[:, cols], in_=half_tanh[:, c, :], func=ACT.Copy, scale=0.5, bias=0.5)
 
-        v_got = {}
-        v_got[0, 0] = gather_values(0, 0)
-        nc.scalar.activation(out=vs_got[:], in_=vs_pool[:].indirect(offsets[:]), func=ACT.Copy)
-        for b in range(B):
-            nc.sync.dma_start(out=vs_cols[:, b, 0:PACK], in_=vs_got[VS_ROW : VS_ROW + 1, b * N : (b + 1) * N])
         first_woven = sb("first_woven", [P, DV, PACK], BF16)
         turn_values(v_got[0, 0], 7, first_woven[:, 0:P, :], nc.scalar.copy)
         sink_turned = psum.tile([P, P], F32, name="sink_turned", tag="bank6")
         nc.tensor.transpose(sink_turned[:], sink_rows[:], ident[:])
-        nc.scalar.activation(out=neg_logits[:, :, N], in_=sink_turned[:, 0:TILES], func=ACT.Copy, scale=-1.0)
+        nc.scalar.activation(out=neg_logits[:, :, N], in_=sink_turned[:, SINK_ROW : SINK_ROW + TILES], func=ACT.Copy, scale=-1.0)
         v_got[0, 1] = gather_values(0, 1)
         accs = [scores(b, h, k_codes[b]) for b in range(B) for h in range(HALVES)]
         soft = [softmax(j, accs[j]) for j in range(TILES)]
         v_got[1, 0] = gather_values(1, 0, tag=f"neg_max{TILES - 1}")
         v_got[1, 1] = gather_values(1, 1, tag="neg_logits")
-        last_woven = sb("last_woven", [P, P, PACK], BF16)
-        make_gate(range(HALVES), tag="k_pool")
+        last_woven = sb("last_woven", [P, P, PACK], BF16, tag="k_codes0")
+        make_gate(range(HALVES), tag="k_pool1")
         turn_values(v_got[1, 1], 0, last_woven[:], nc.scalar.copy)
         make_gate(range(HALVES, TILES), tag="neg_logits")
         nc.vector.reciprocal(inverses[:], totals[:])

@@ -30,6 +30,7 @@ PLANES = DV // P
 QUADS = (0, 2, 1, 3)
 VS_ROW = 16
 SINK_ROW = 24
+EARLY = T // 4
 
 
 def tile_attend_soft_sink_gate_segb2q256n512t2048_kernel(
@@ -54,12 +55,14 @@ def tile_attend_soft_sink_gate_segb2q256n512t2048_kernel(
         totals = sb("totals", [P, TILES], F32)
         inverses = sb("inverses", [P, TILES], F32)
 
+        minus_one = sb("minus_one", [P, TILES], F32)
         nc.gpsimd.memset(ident[:], 0.0)
-        nc.vector.memset(vs_pool[:, 0:SEG].bitcast(I32), 0)
-        nc.gpsimd.memset(vs_pool[:, SEG:T].bitcast(I32), 0)
+        nc.vector.memset(vs_pool[:, 0 : T - EARLY].bitcast(I32), 0)
+        nc.gpsimd.memset(vs_pool[:, T - EARLY : T].bitcast(I32), 0)
         nc.vector.memset(ks_pool[0:KS_ROW0, :].bitcast(I32), 0)
         nc.scalar.activation(out=sink_rows[:], in_=ident[:], func=ACT.Copy)
         make_identity(nc, ident[:], nomemset=True)
+        nc.gpsimd.memset(minus_one[:], -1.0)
 
         k_flat = k_words[0].rearrange("p t r -> p (t r)").bitcast(I32)
         v_pool, q_codes, k_pool, k_got, k_codes, k_planes = {}, {}, {}, {}, {}, {}
@@ -113,20 +116,21 @@ def tile_attend_soft_sink_gate_segb2q256n512t2048_kernel(
         def gather_token_scales(b, tag=""):
             vs_got = sb(f"vs_got{b}", [P, N], F32, tag=tag)
             nc.scalar.activation(out=vs_got[:], in_=vs_pool[:].indirect(listed(b)), func=ACT.Copy)
-            nc.sync.dma_start(out=vs_cols[:, b, 0:PACK], in_=vs_got[VS_ROW : VS_ROW + 1, :])
+            vs_cols[b] = sb(f"vs_cols{b}", [P, 8], F32, tag=f"ks_got{b}")
+            nc.sync.dma_start(out=vs_cols[b][:, 0:PACK], in_=vs_got[VS_ROW : VS_ROW + 1, :])
 
         nc.sync.dma_start(offsets[:], offs)
         nc.sync.dma_start(
             out=ks_pool[KS_ROW0:P, :].bitcast(I32), in_=k_scales.rearrange("o f t -> f o t").bitcast(I32)
         )
         load_keys(0)
-        nc.sync.dma_start(out=vs_pool[VS_ROW : VS_ROW + 1, :], in_=vs[0:1, :])
-        load_values(0, 0)
         for quad in QUADS:
             nc.sync.dma_start(
                 out=q_planes[32 * quad : 32 * quad + 4, :].bitcast(I32).rearrange("f (g q) -> f g q", g=B * PASSES),
                 in_=q_scales[:, :, 4 * quad : 4 * quad + 4, :].rearrange("b o f q -> f (b o) q").bitcast(I32),
             )
+        nc.sync.dma_start(out=vs_pool[VS_ROW : VS_ROW + 1, :], in_=vs[0:1, :])
+        load_values(0, 0)
         load_keys(1)
         load_queries(0)
         nc.sync.dma_start(
@@ -143,7 +147,7 @@ def tile_attend_soft_sink_gate_segb2q256n512t2048_kernel(
         gather_keys(1)
         part_keys(1)
         load_values(1, 0, tag="k_got0")
-        vs_cols = sb("vs_cols", [P, B, 8], F32)
+        vs_cols = {}
         gather_token_scales(0)
         v_got = {(0, 0): gather_values(0, 0)}
         gather_token_scales(1, tag="v_pool00")
@@ -215,7 +219,7 @@ def tile_attend_soft_sink_gate_segb2q256n512t2048_kernel(
             nc.vector.tensor_tensor(
                 out=w_woven[b][:, h * P : (h + 1) * P, :],
                 in0=turned[:].rearrange("p t q -> p q t"),
-                in1=vs_cols[:, b, 0:PACK].unsqueeze(1).to_broadcast([P, P, PACK]),
+                in1=vs_cols[b][:, 0:PACK].unsqueeze(1).to_broadcast([P, P, PACK]),
                 op=ALU.mult,
             )
 
@@ -274,7 +278,7 @@ def tile_attend_soft_sink_gate_segb2q256n512t2048_kernel(
         make_gate(range(HALVES), tag="k_pool1")
         turn_values(v_got[1, 1], 0, last_woven[:], nc.scalar.copy)
         make_gate(range(HALVES, TILES), tag="neg_logits")
-        nc.vector.reciprocal(inverses[:], totals[:])
+        nc.gpsimd.tensor_tensor(out=inverses[:], in0=totals[:], in1=minus_one[:], op=ALU.pow)
         w_woven = [sb(f"w_woven{b}", [P, NQ, PACK], BF16) for b in range(B)]
         for j in range(TILES):
             weigh(j, soft[j])

@@ -30,7 +30,6 @@ PLANES = DV // P
 QUADS = (0, 2, 1, 3)
 VS_ROW = 16
 SINK_ROW = 24
-EARLY = T // 4
 
 
 def tile_attend_soft_sink_gate_segb2q256n512t2048_kernel(
@@ -56,12 +55,12 @@ def tile_attend_soft_sink_gate_segb2q256n512t2048_kernel(
         inverses = sb("inverses", [P, TILES], F32)
 
         minus_one = sb("minus_one", [P, TILES], F32)
-        nc.gpsimd.memset(ident[:], 0.0)
-        nc.vector.memset(vs_pool[:, 0 : T - EARLY].bitcast(I32), 0)
-        nc.gpsimd.memset(vs_pool[:, T - EARLY : T].bitcast(I32), 0)
+        zeros = sb("zeros", [P, 8], F32)
+        nc.gpsimd.memset(zeros[:], 0.0)
+        make_identity(nc, ident[:])
+        nc.vector.memset(vs_pool[:].bitcast(I32), 0)
         nc.vector.memset(ks_pool[0:KS_ROW0, :].bitcast(I32), 0)
-        nc.scalar.activation(out=sink_rows[:], in_=ident[:], func=ACT.Copy)
-        make_identity(nc, ident[:], nomemset=True)
+        nc.scalar.activation(out=sink_rows[:], in_=zeros[:, 0:1].to_broadcast([P, P]), func=ACT.Copy)
         nc.gpsimd.memset(minus_one[:], -1.0)
 
         k_flat = k_words[0].rearrange("p t r -> p (t r)").bitcast(I32)
@@ -283,7 +282,7 @@ def tile_attend_soft_sink_gate_segb2q256n512t2048_kernel(
         for j in range(TILES):
             weigh(j, soft[j])
         turn_values(v_got[0, 1], 2, first_woven[:, P:DV, :], nc.vector.tensor_copy)
-        w_mx = [quantize(f"w{b}", w_woven[b], NQ) for b in range(B)]
+        w_mx = [quantize("w0", w_woven[0], NQ, tag=f"probs{TILES - 1}"), quantize("w1", w_woven[1], NQ)]
         third_woven = sb("third_woven", [P, P, PACK], BF16, tag="w_woven0")
         turn_values(v_got[1, 0], 3, third_woven[:], nc.vector.tensor_copy)
         second_woven = [third_woven, last_woven]

@@ -183,8 +183,8 @@ def tile_attend_soft_sink_gate_segb2q256n512t2048_kernel(
         def softmax(j, acc):
             neg_max = sb(f"neg_max{j}", [P, 1], F32)
             nc.vector.tensor_scalar(
-                out=neg_logits[:, j, 0:N].rearrange("p (t s) -> p s t", t=PACK),
-                in0=acc[:].rearrange("p (s t) -> p s t", t=PACK),
+                out=neg_logits[:, j, 0:N].rearrange("p (t s) -> p t s", t=PACK),
+                in0=acc[:].rearrange("p (s t) -> p t s", t=PACK),
                 scalar1=-1.0,
                 scalar2=neg_logits[:, j, N : N + 1],
                 op0=ALU.mult,

@@ -38,10 +38,14 @@ def tile_attend_soft_sink_gate_segb2q256n512t2048_kernel(
     nc = tc.nc
     with ExitStack() as ctx:
         keep = ctx.enter_context(tc.tile_pool(name="keep", bufs=1))
+        shared = ctx.enter_context(tc.tile_pool(name="shared", bufs=1))
         psum = ctx.enter_context(tc.psum_pool(name="psum", bufs=1))
 
         def sb(name, shape, dtype, tag=""):
             return keep.tile(shape, dtype, name=name, tag=tag or name, align_bytes=64)
+
+        def placed(name, shape, dtype, offset):
+            return shared.tile(shape, dtype, name=name, tag=name, align_bytes=64, offset=offset)
 
         offsets = keep.tile([P, B * LIST_COLS], U16, name="offsets")
         ks_pool = sb("ks_pool", [P, T], U8)
@@ -84,7 +88,7 @@ def tile_attend_soft_sink_gate_segb2q256n512t2048_kernel(
             return offsets[:, b * LIST_COLS : (b + 1) * LIST_COLS]
 
         def gather_key_scales(b):
-            ks_got = sb(f"ks_got{b}", [P, N], U8)
+            ks_got = placed(f"ks_got{b}", [P, N], U8, b * N)
             nc.vector.tensor_copy(ks_got[:], ks_pool[:].indirect(listed(b)))
             return ks_got
 
@@ -115,7 +119,7 @@ def tile_attend_soft_sink_gate_segb2q256n512t2048_kernel(
         def gather_token_scales(b, tag=""):
             vs_got = sb(f"vs_got{b}", [P, N], F32, tag=tag)
             nc.scalar.activation(out=vs_got[:], in_=vs_pool[:].indirect(listed(b)), func=ACT.Copy)
-            vs_cols[b] = sb(f"vs_cols{b}", [P, 8], F32, tag=f"ks_got{b}")
+            vs_cols[b] = placed(f"vs_cols{b}", [P, 8], F32, b * N)
             nc.sync.dma_start(out=vs_cols[b][:, 0:PACK], in_=vs_got[VS_ROW : VS_ROW + 1, :])
 
         nc.sync.dma_start(offsets[:], offs)
@@ -130,11 +134,11 @@ def tile_attend_soft_sink_gate_segb2q256n512t2048_kernel(
             )
         nc.sync.dma_start(out=vs_pool[VS_ROW : VS_ROW + 1, :], in_=vs[0:1, :])
         load_values(0, 0)
-        load_keys(1)
-        load_queries(0)
         nc.sync.dma_start(
             out=sink_rows[SINK_ROW : SINK_ROW + TILES, :], in_=sink.rearrange("b (h p) one -> (b h) (p one)", p=P)
         )
+        load_keys(1)
+        load_queries(0)
 
         move_key_scales(0, gather_key_scales(0))
         gather_keys(0)
@@ -191,7 +195,7 @@ def tile_attend_soft_sink_gate_segb2q256n512t2048_kernel(
                 op1=ALU.min,
                 accum_out=neg_max[:],
             )
-            probs = sb(f"probs{j}", [P, ROW], F32)
+            probs = sb(f"probs{j}", [P, ROW], F32) if j else placed("probs0", [P, ROW], F32, N + 64)
             nc.scalar.activation(
                 out=probs[:, 0 : N + 1],
                 in_=neg_logits[:, j, 0 : N + 1],
@@ -200,7 +204,7 @@ def tile_attend_soft_sink_gate_segb2q256n512t2048_kernel(
                 scale=-1.0,
                 accum_out=totals[:, j : j + 1],
             )
-            turned = psum.tile([P, PACK, P], F32, name="probs_turned", tag=f"bank{(j + HALVES) % TILES}")
+            turned = psum.tile([P, PACK, P], F32, name="probs_turned", tag=f"bank{(j + 1) % TILES}")
             for t in range(PACK):
                 nc.tensor.transpose(turned[:, t, :], probs[:, t * P : (t + 1) * P], ident[:])
             return turned
@@ -222,21 +226,22 @@ def tile_attend_soft_sink_gate_segb2q256n512t2048_kernel(
                 op=ALU.mult,
             )
 
-        def mix(j, w_mx, v_parts):
-            rows = slice(j % HALVES * P, (j % HALVES + 1) * P)
-            acc = psum.tile([P, DV], F32, name="mixed", tag=f"bank{4 + j}")
+        def mix(b, w_mx, v_parts):
+            accs = [psum.tile([P, DV], F32, name="mixed", tag=f"bank{4 + b * HALVES + h}") for h in range(HALVES)]
             width = DV // len(v_parts)
             for c, v_mx in enumerate(v_parts):
-                nc.tensor.matmul_mx(
-                    out=acc[:, c * width : (c + 1) * width],
-                    lhsT=w_mx[0][:, rows].bitcast(FP8X4),
-                    lhsT_scale=w_mx[1][:, rows],
-                    rhs=v_mx[0][:].bitcast(FP8X4),
-                    rhs_scale=v_mx[1][:],
-                    start=True,
-                    stop=True,
-                )
-            return acc
+                for h in range(HALVES):
+                    rows = slice(h * P, (h + 1) * P)
+                    nc.tensor.matmul_mx(
+                        out=accs[h][:, c * width : (c + 1) * width],
+                        lhsT=w_mx[0][:, rows].bitcast(FP8X4),
+                        lhsT_scale=w_mx[1][:, rows],
+                        rhs=v_mx[0][:].bitcast(FP8X4),
+                        rhs_scale=v_mx[1][:],
+                        start=True,
+                        stop=True,
+                    )
+            return accs
 
         def finish(j, acc):
             result = sb(f"result{j}", [P, DV], F32)
@@ -275,21 +280,21 @@ def tile_attend_soft_sink_gate_segb2q256n512t2048_kernel(
         v_got[1, 1] = gather_values(1, 1, tag="neg_logits")
         last_woven = sb("last_woven", [P, P, PACK], BF16, tag="k_codes0")
         make_gate(range(HALVES), tag="k_pool1")
-        turn_values(v_got[1, 1], 0, last_woven[:], nc.scalar.copy)
+        turn_values(v_got[1, 1], 3, last_woven[:], nc.scalar.copy)
         make_gate(range(HALVES, TILES), tag="neg_logits")
         nc.gpsimd.tensor_tensor(out=inverses[:], in0=totals[:], in1=minus_one[:], op=ALU.pow)
         w_woven = [sb(f"w_woven{b}", [P, NQ, PACK], BF16) for b in range(B)]
         for j in range(TILES):
             weigh(j, soft[j])
-        turn_values(v_got[0, 1], 2, first_woven[:, P:DV, :], nc.vector.tensor_copy)
+        turn_values(v_got[0, 1], 1, first_woven[:, P:DV, :], nc.vector.tensor_copy)
         w_mx = [quantize("w0", w_woven[0], NQ, tag=f"probs{TILES - 1}"), quantize("w1", w_woven[1], NQ)]
         third_woven = sb("third_woven", [P, P, PACK], BF16, tag="w_woven0")
-        turn_values(v_got[1, 0], 3, third_woven[:], nc.vector.tensor_copy)
+        turn_values(v_got[1, 0], 2, third_woven[:], nc.vector.tensor_copy)
         second_woven = [third_woven, last_woven]
         v_mx = [
             [quantize("v0", first_woven, DV)],
             [quantize(f"v1{h}", second_woven[h], P) for h in range(PLANES)],
         ]
-        mixed = [mix(j, w_mx[j // HALVES], v_mx[j // HALVES]) for j in range(TILES)]
+        mixed = [acc for b in range(B) for acc in mix(b, w_mx[b], v_mx[b])]
         for j in range(TILES):
             finish(j, mixed[j])

@@ -56,7 +56,6 @@ def tile_attend_soft_sink_gate_segb2q256n512t2048_kernel(
         gate = sb("gate", [P, TILES * DV], F32)
         ident = sb("ident", [P, P], F32)
         totals = sb("totals", [P, TILES], F32)
-        inverses = sb("inverses", [P, TILES], F32)
 
         minus_one = sb("minus_one", [P, TILES], F32)
         zeros = sb("zeros", [P, 8], F32)
@@ -276,20 +275,24 @@ def tile_attend_soft_sink_gate_segb2q256n512t2048_kernel(
         v_got[0, 1] = gather_values(0, 1)
         accs = [scores(b, h, k_codes[b]) for b in range(B) for h in range(HALVES)]
         soft = [softmax(j, accs[j]) for j in range(TILES)]
-        v_got[1, 0] = gather_values(1, 0, tag=f"neg_max{TILES - 1}")
+        v_got[1, 0] = sb("v_got10", [P, N], BF16, tag=f"neg_max{TILES - 1}")
+        shares = [listed(1)[:, c * LIST_COLS // 2 : (c + 1) * LIST_COLS // 2] for c in range(2)]
+        nc.scalar.activation(out=v_got[1, 0][:, 0 : N // 2], in_=v_pool[1, 0][:].indirect(shares[0]), func=ACT.Copy)
+        nc.vector.tensor_copy(v_got[1, 0][:, N // 2 : N], v_pool[1, 0][:].indirect(shares[1]))
         v_got[1, 1] = gather_values(1, 1, tag="neg_logits")
-        last_woven = sb("last_woven", [P, P, PACK], BF16, tag="k_codes0")
-        make_gate(range(HALVES), tag="k_pool1")
+        turn_values(v_got[0, 1], 1, first_woven[:, P:DV, :], nc.scalar.copy)
+        third_woven = sb("third_woven", [P, P, PACK], BF16)
+        turn_values(v_got[1, 0], 2, third_woven[:], nc.scalar.copy)
+        make_gate(range(1), tag="k_pool1")
+        last_woven = sb("last_woven", [P, P, PACK], BF16)
         turn_values(v_got[1, 1], 3, last_woven[:], nc.scalar.copy)
-        make_gate(range(HALVES, TILES), tag="neg_logits")
+        make_gate(range(1, TILES), tag="neg_logits")
+        inverses = sb("inverses", [P, TILES], F32, tag="k_got0")
         nc.gpsimd.tensor_tensor(out=inverses[:], in0=totals[:], in1=minus_one[:], op=ALU.pow)
         w_woven = [sb(f"w_woven{b}", [P, NQ, PACK], BF16) for b in range(B)]
         for j in range(TILES):
             weigh(j, soft[j])
-        turn_values(v_got[0, 1], 1, first_woven[:, P:DV, :], nc.vector.tensor_copy)
         w_mx = [quantize("w0", w_woven[0], NQ, tag=f"probs{TILES - 1}"), quantize("w1", w_woven[1], NQ)]
-        third_woven = sb("third_woven", [P, P, PACK], BF16, tag="w_woven0")
-        turn_values(v_got[1, 0], 2, third_woven[:], nc.vector.tensor_copy)
         second_woven = [third_woven, last_woven]
         v_mx = [
             [quantize("v0", first_woven, DV)],

@@ -30,6 +30,7 @@ PLANES = DV // P
 QUADS = (0, 2, 1, 3)
 VS_ROW = 16
 SINK_ROW = 24
+PROB_BANKS = (2, 1, 3, 0)
 
 
 def tile_attend_soft_sink_gate_segb2q256n512t2048_kernel(
@@ -118,6 +119,9 @@ def tile_attend_soft_sink_gate_segb2q256n512t2048_kernel(
         def gather_token_scales(b, tag=""):
             vs_got = sb(f"vs_got{b}", [P, N], F32, tag=tag)
             nc.scalar.activation(out=vs_got[:], in_=vs_pool[:].indirect(listed(b)), func=ACT.Copy)
+            return vs_got
+
+        def move_token_scales(b, vs_got):
             vs_cols[b] = placed(f"vs_cols{b}", [P, 8], F32, b * N)
             nc.sync.dma_start(out=vs_cols[b][:, 0:PACK], in_=vs_got[VS_ROW : VS_ROW + 1, :])
 
@@ -150,13 +154,20 @@ def tile_attend_soft_sink_gate_segb2q256n512t2048_kernel(
         part_keys(1)
         load_values(1, 0, tag="k_got0")
         vs_cols = {}
-        gather_token_scales(0)
+        move_token_scales(0, gather_token_scales(0))
         v_got = {(0, 0): gather_values(0, 0)}
-        gather_token_scales(1, tag="v_pool00")
+        second_row = gather_token_scales(1, tag="v_pool00")
         load_values(1, 1, tag="k_pool1")
+        move_token_scales(1, second_row)
         og_sb = [sb(f"og{b}", [P, HALVES, DV], F32, tag=f"k_codes{b}") for b in range(B)]
         for b in range(B):
             nc.sync.dma_start(out=og_sb[b][:], in_=og[b].rearrange("(h p) e -> p h e", p=P))
+
+        def share_values(b, h, tag):
+            v_got = sb(f"v_got{b}{h}", [P, N], BF16, tag=tag)
+            shares = [listed(b)[:, c * LIST_COLS // 2 : (c + 1) * LIST_COLS // 2] for c in range(2)]
+            nc.scalar.activation(out=v_got[:, 0 : N // 2], in_=v_pool[b, h][:].indirect(shares[0]), func=ACT.Copy)
+            return v_got, lambda: nc.vector.tensor_copy(v_got[:, N // 2 : N], v_pool[b, h][:].indirect(shares[1]))
 
         def turn_values(got, bank, woven, copy):
             turned = psum.tile([P, 2, P], F32, name="v_turned", tag=f"bank{bank}")
@@ -194,7 +205,7 @@ def tile_attend_soft_sink_gate_segb2q256n512t2048_kernel(
                 op1=ALU.min,
                 accum_out=neg_max[:],
             )
-            probs = sb(f"probs{j}", [P, ROW], F32) if j else placed("probs0", [P, ROW], F32, N + 64)
+            probs = placed("probs1", [P, ROW], F32, N + 64) if j == 1 else sb(f"probs{j}", [P, ROW], F32)
             nc.scalar.activation(
                 out=probs[:, 0 : N + 1],
                 in_=neg_logits[:, j, 0 : N + 1],
@@ -203,7 +214,7 @@ def tile_attend_soft_sink_gate_segb2q256n512t2048_kernel(
                 scale=-1.0,
                 accum_out=totals[:, j : j + 1],
             )
-            turned = psum.tile([P, PACK, P], F32, name="probs_turned", tag=f"bank{(j + 1) % TILES}")
+            turned = psum.tile([P, PACK, P], F32, name="probs_turned", tag=f"bank{PROB_BANKS[j]}")
             for t in range(PACK):
                 nc.tensor.transpose(turned[:, t, :], probs[:, t * P : (t + 1) * P], ident[:])
             return turned
@@ -272,13 +283,13 @@ def tile_attend_soft_sink_gate_segb2q256n512t2048_kernel(
         sink_turned = psum.tile([P, P], F32, name="sink_turned", tag="bank6")
         nc.tensor.transpose(sink_turned[:], sink_rows[:], ident[:])
         nc.scalar.activation(out=neg_logits[:, :, N], in_=sink_turned[:, SINK_ROW : SINK_ROW + TILES], func=ACT.Copy, scale=-1.0)
-        v_got[0, 1] = gather_values(0, 1)
+        v_got[0, 1], vector_share = share_values(0, 1, "k_got1")
         accs = [scores(b, h, k_codes[b]) for b in range(B) for h in range(HALVES)]
-        soft = [softmax(j, accs[j]) for j in range(TILES)]
-        v_got[1, 0] = sb("v_got10", [P, N], BF16, tag=f"neg_max{TILES - 1}")
-        shares = [listed(1)[:, c * LIST_COLS // 2 : (c + 1) * LIST_COLS // 2] for c in range(2)]
-        nc.scalar.activation(out=v_got[1, 0][:, 0 : N // 2], in_=v_pool[1, 0][:].indirect(shares[0]), func=ACT.Copy)
-        nc.vector.tensor_copy(v_got[1, 0][:, N // 2 : N], v_pool[1, 0][:].indirect(shares[1]))
+        soft = [softmax(0, accs[0])]
+        vector_share()
+        soft.extend(softmax(j, accs[j]) for j in range(1, TILES))
+        v_got[1, 0], vector_share = share_values(1, 0, f"neg_max{TILES - 1}")
+        vector_share()
         v_got[1, 1] = gather_values(1, 1, tag="neg_logits")
         turn_values(v_got[0, 1], 1, first_woven[:, P:DV, :], nc.scalar.copy)
         third_woven = sb("third_woven", [P, P, PACK], BF16)

@@ -30,7 +30,10 @@ PLANES = DV // P
 QUADS = (0, 2, 1, 3)
 VS_ROW = 16
 SINK_ROW = 24
+EARLY = 2 * N + 4 * (N + 16)
+SECOND_GOT = 16384
 PROB_BANKS = (2, 1, 3, 0)
+MIX_BANKS = (3, 5, 6, 7)
 
 
 def tile_attend_soft_sink_gate_segb2q256n512t2048_kernel(
@@ -71,7 +74,10 @@ def tile_attend_soft_sink_gate_segb2q256n512t2048_kernel(
         v_pool, q_codes, k_pool, k_got, k_codes, k_planes = {}, {}, {}, {}, {}, {}
 
         def load_values(b, h, tag=""):
-            v_pool[b, h] = sb(f"v_pool{b}{h}", [P, (b + 1) * SEG], F32, tag=tag)
+            if (b, h) == (1, 0):
+                v_pool[b, h] = placed("v_pool10", [P, T], F32, EARLY + 4 * DV)
+            else:
+                v_pool[b, h] = sb(f"v_pool{b}{h}", [P, (b + 1) * SEG], F32, tag=tag)
             nc.sync.dma_start(
                 out=v_pool[b, h][:, b * SEG : (b + 1) * SEG], in_=vT[h * P : (h + 1) * P, b * SEG : (b + 1) * SEG]
             )
@@ -101,7 +107,7 @@ def tile_attend_soft_sink_gate_segb2q256n512t2048_kernel(
                 )
 
         def gather_keys(b):
-            k_got[b] = sb(f"k_got{b}", [P, N], U32)
+            k_got[b] = placed("k_got1", [P, N], U32, SECOND_GOT) if b else placed("k_got0", [P, N], U32, EARLY)
             nc.vector.tensor_copy(k_got[b][:], k_pool[b][:].bitcast(U32).indirect(listed(b)))
 
         def part_keys(b):
@@ -152,19 +158,21 @@ def tile_attend_soft_sink_gate_segb2q256n512t2048_kernel(
         part_keys(0)
         gather_keys(1)
         part_keys(1)
-        load_values(1, 0, tag="k_got0")
+        og_rows = og.rearrange("b (h p) e -> p (b h) e", p=P)
+        og_first = placed("og_first", [P, 1, DV], F32, EARLY)
+        nc.sync.dma_start(out=og_first[:], in_=og_rows[:, 0:1, :])
+        load_values(1, 0)
         vs_cols = {}
         move_token_scales(0, gather_token_scales(0))
         v_got = {(0, 0): gather_values(0, 0)}
         second_row = gather_token_scales(1, tag="v_pool00")
         load_values(1, 1, tag="k_pool1")
         move_token_scales(1, second_row)
-        og_sb = [sb(f"og{b}", [P, HALVES, DV], F32, tag=f"k_codes{b}") for b in range(B)]
-        for b in range(B):
-            nc.sync.dma_start(out=og_sb[b][:], in_=og[b].rearrange("(h p) e -> p h e", p=P))
+        og_rest = sb("og_rest", [P, TILES - 1, DV], F32, tag="k_codes0")
+        nc.sync.dma_start(out=og_rest[:], in_=og_rows[:, 1:TILES, :])
+        og_sb = [og_first[:, 0, :]] + [og_rest[:, j, :] for j in range(TILES - 1)]
 
-        def share_values(b, h, tag):
-            v_got = sb(f"v_got{b}{h}", [P, N], BF16, tag=tag)
+        def share_values(b, h, v_got):
             shares = [listed(b)[:, c * LIST_COLS // 2 : (c + 1) * LIST_COLS // 2] for c in range(2)]
             nc.scalar.activation(out=v_got[:, 0 : N // 2], in_=v_pool[b, h][:].indirect(shares[0]), func=ACT.Copy)
             return v_got, lambda: nc.vector.tensor_copy(v_got[:, N // 2 : N], v_pool[b, h][:].indirect(shares[1]))
@@ -237,7 +245,7 @@ def tile_attend_soft_sink_gate_segb2q256n512t2048_kernel(
             )
 
         def mix(b, w_mx, v_parts):
-            accs = [psum.tile([P, DV], F32, name="mixed", tag=f"bank{4 + b * HALVES + h}") for h in range(HALVES)]
+            accs = [psum.tile([P, DV], F32, name="mixed", tag=f"bank{MIX_BANKS[b * HALVES + h]}") for h in range(HALVES)]
             width = DV // len(v_parts)
             for c, v_mx in enumerate(v_parts):
                 for h in range(HALVES):
@@ -269,7 +277,7 @@ def tile_attend_soft_sink_gate_segb2q256n512t2048_kernel(
         def make_gate(tiles, tag):
             half_tanh = sb(f"half_tanh{tiles[0]}", [P, len(tiles), DV], F32, tag=tag)
             for c, j in enumerate(tiles):
-                nc.scalar.activation(out=half_tanh[:, c, :], in_=og_sb[j // HALVES][:, j % HALVES, :], func=ACT.Tanh, scale=0.5)
+                nc.scalar.activation(out=half_tanh[:, c, :], in_=og_sb[j], func=ACT.Tanh, scale=0.5)
                 cols = slice(j * DV, (j + 1) * DV)
                 if j < TILES - 1:
                     nc.gpsimd.tensor_scalar(
@@ -278,35 +286,50 @@ def tile_attend_soft_sink_gate_segb2q256n512t2048_kernel(
                 else:
                     nc.scalar.activation(out=gate[:, cols], in_=half_tanh[:, c, :], func=ACT.Copy, scale=0.5, bias=0.5)
 
-        first_woven = sb("first_woven", [P, DV, PACK], BF16)
-        turn_values(v_got[0, 0], 7, first_woven[:, 0:P, :], nc.scalar.copy)
+        first_woven = [sb(f"first_woven{h}", [P, P, PACK], BF16) for h in range(PLANES)]
+        turn_values(v_got[0, 0], 7, first_woven[0][:], nc.scalar.copy)
+        first_codes = placed("first_codes", [P, DV], U32, SECOND_GOT + 2 * N)
+        first_plane = sb("first_plane", [P, DV], U8)
+
+        def quantize_first(h):
+            cols = slice(h * P, (h + 1) * P)
+            nc.vector.quantize_mx(
+                out=first_codes[:, cols].bitcast(FP8X4),
+                scales=first_plane[:, cols],
+                in_=first_woven[h][:].rearrange("p c t -> p (c t)"),
+            )
+
+        quantize_first(0)
         sink_turned = psum.tile([P, P], F32, name="sink_turned", tag="bank6")
         nc.tensor.transpose(sink_turned[:], sink_rows[:], ident[:])
         nc.scalar.activation(out=neg_logits[:, :, N], in_=sink_turned[:, SINK_ROW : SINK_ROW + TILES], func=ACT.Copy, scale=-1.0)
-        v_got[0, 1], vector_share = share_values(0, 1, "k_got1")
+        v_got[0, 1], vector_share = share_values(0, 1, placed("v_got01", [P, N], BF16, SECOND_GOT))
         accs = [scores(b, h, k_codes[b]) for b in range(B) for h in range(HALVES)]
         soft = [softmax(0, accs[0])]
         vector_share()
+        make_gate(range(1), tag="")
         soft.extend(softmax(j, accs[j]) for j in range(1, TILES))
-        v_got[1, 0], vector_share = share_values(1, 0, f"neg_max{TILES - 1}")
+        v_got[1, 0], vector_share = share_values(1, 0, sb("v_got10", [P, N], BF16, tag="neg_max1"))
         vector_share()
-        v_got[1, 1] = gather_values(1, 1, tag="neg_logits")
-        turn_values(v_got[0, 1], 1, first_woven[:, P:DV, :], nc.scalar.copy)
+        v_got[1, 1] = gather_values(1, 1, tag="neg_max2")
+        turn_values(v_got[0, 1], 1, first_woven[1][:], nc.scalar.copy)
         third_woven = sb("third_woven", [P, P, PACK], BF16)
         turn_values(v_got[1, 0], 2, third_woven[:], nc.scalar.copy)
-        make_gate(range(1), tag="k_pool1")
+        make_gate(range(1, 2), tag="k_pool1")
         last_woven = sb("last_woven", [P, P, PACK], BF16)
         turn_values(v_got[1, 1], 3, last_woven[:], nc.scalar.copy)
-        make_gate(range(1, TILES), tag="neg_logits")
-        inverses = sb("inverses", [P, TILES], F32, tag="k_got0")
+        make_gate(range(HALVES, TILES), tag="neg_max2")
+        inverses = placed("inverses", [P, TILES], F32, EARLY + 4 * DV)
         nc.gpsimd.tensor_tensor(out=inverses[:], in0=totals[:], in1=minus_one[:], op=ALU.pow)
         w_woven = [sb(f"w_woven{b}", [P, NQ, PACK], BF16) for b in range(B)]
         for j in range(TILES):
             weigh(j, soft[j])
-        w_mx = [quantize("w0", w_woven[0], NQ, tag=f"probs{TILES - 1}"), quantize("w1", w_woven[1], NQ)]
+        w_mx = [quantize("w0", w_woven[0], NQ, tag=f"probs{TILES - 1}")]
+        quantize_first(1)
+        w_mx.append(quantize("w1", w_woven[1], NQ))
         second_woven = [third_woven, last_woven]
         v_mx = [
-            [quantize("v0", first_woven, DV)],
+            [(first_codes, first_plane)],
             [quantize(f"v1{h}", second_woven[h], P) for h in range(PLANES)],
         ]
         mixed = [acc for b in range(B) for acc in mix(b, w_mx[b], v_mx[b])]

from contextlib import ExitStack

import concourse.mybir as mybir
from concourse.masks import make_identity

B, N, T, D, DV, NQ = 2, 512, 2048, 1024, 256, 256
FLOPS = 2 * B * NQ * N * (D + DV)

F32 = mybir.dt.float32
BF16 = mybir.dt.bfloat16
I32 = mybir.dt.int32
U32 = mybir.dt.uint32
U16 = mybir.dt.uint16
U8 = mybir.dt.uint8
FP8X4 = mybir.dt.float8_e4m3fn_x4
FP4X4 = mybir.dt.float4_e2m1fn_x4
ALU = mybir.AluOpType
ACT = mybir.ActivationFunctionType

P = 128
PACK = 4
PASSES = D // (P * PACK)
SEG = T // B
HALVES = NQ // P
TILES = B * HALVES
LIST_COLS = N // 16
ROW = N + 8
KS_ROW0 = 96
PLANES = DV // P
QUADS = (0, 2, 1, 3)
VS_ROW = 16
SINK_ROW = 24
EARLY = 2 * N + 4 * (N + 16)
SECOND_GOT = 16384
PROB_BANKS = (2, 1, 3, 0)
MIX_BANKS = (3, 5, 6, 7)


def tile_attend_soft_sink_gate_segb2q256n512t2048_kernel(
    tc, q_words, q_scales, k_words, k_scales, vT, vs, sink, og, offs, out
):
    nc = tc.nc
    with ExitStack() as ctx:
        keep = ctx.enter_context(tc.tile_pool(name="keep", bufs=1))
        shared = ctx.enter_context(tc.tile_pool(name="shared", bufs=1))
        psum = ctx.enter_context(tc.psum_pool(name="psum", bufs=1))

        def sb(name, shape, dtype, tag=""):
            return keep.tile(shape, dtype, name=name, tag=tag or name, align_bytes=64)

        def placed(name, shape, dtype, offset):
            return shared.tile(shape, dtype, name=name, tag=name, align_bytes=64, offset=offset)

        offsets = keep.tile([P, B * LIST_COLS], U16, name="offsets")
        ks_pool = sb("ks_pool", [P, T], U8)
        vs_pool = sb("vs_pool", [P, T], F32)
        neg_logits = sb("neg_logits", [P, TILES, ROW], F32)
        q_planes = sb("q_planes", [P, B * PASSES * NQ], U8)
        sink_rows = sb("sink_rows", [P, P], F32)
        gate = sb("gate", [P, TILES * DV], F32)
        ident = sb("ident", [P, P], F32)
        totals = sb("totals", [P, TILES], F32)

        minus_one = sb("minus_one", [P, TILES], F32)
        zeros = sb("zeros", [P, 8], F32)
        nc.gpsimd.memset(zeros[:], 0.0)
        make_identity(nc, ident[:])
        nc.vector.memset(vs_pool[:].bitcast(I32), 0)
        nc.vector.memset(ks_pool[0:KS_ROW0, :].bitcast(I32), 0)
        nc.scalar.activation(out=sink_rows[:], in_=zeros[:, 0:1].to_broadcast([P, P]), func=ACT.Copy)
        nc.gpsimd.memset(minus_one[:], -1.0)

        k_flat = k_words[0].rearrange("p t r -> p (t r)").bitcast(I32)
        v_pool, q_codes, k_pool, k_got, k_codes, k_planes = {}, {}, {}, {}, {}, {}

        def load_values(b, h, tag=""):
            if (b, h) == (1, 0):
                v_pool[b, h] = placed("v_pool10", [P, T], F32, EARLY + 4 * DV)
            else:
                v_pool[b, h] = sb(f"v_pool{b}{h}", [P, (b + 1) * SEG], F32, tag=tag)
            nc.sync.dma_start(
                out=v_pool[b, h][:, b * SEG : (b + 1) * SEG], in_=vT[h * P : (h + 1) * P, b * SEG : (b + 1) * SEG]
            )

        def load_keys(b):
            k_pool[b] = sb(f"k_pool{b}", [P, (b + 1) * SEG], I32)
            nc.sync.dma_start(out=k_pool[b][:, b * SEG : (b + 1) * SEG], in_=k_flat[:, b * SEG : (b + 1) * SEG])

        def load_queries(b, tag=""):
            q_codes[b] = sb(f"q_codes{b}", [P, PASSES, NQ], I32, tag=tag)
            nc.sync.dma_start(out=q_codes[b][:], in_=q_words[b].rearrange("o p q r -> p o (q r)").bitcast(I32))

        def listed(b):
            return offsets[:, b * LIST_COLS : (b + 1) * LIST_COLS]

        def gather_key_scales(b):
            ks_got = placed(f"ks_got{b}", [P, N], U8, b * N)
            nc.vector.tensor_copy(ks_got[:], ks_pool[:].indirect(listed(b)))
            return ks_got

        def move_key_scales(b, ks_got):
            k_planes[b] = sb(f"k_planes{b}", [P, PASSES * N], U8)
            for quad in QUADS:
                nc.sync.dma_start(
                    out=k_planes[b][32 * quad : 32 * quad + 4, :].bitcast(I32).rearrange("f (o n) -> f o n", o=PASSES),
                    in_=ks_got[KS_ROW0 + 8 * quad : KS_ROW0 + 8 * quad + 8, :].bitcast(I32),
                )

        def gather_keys(b):
            k_got[b] = placed("k_got1", [P, N], U32, SECOND_GOT) if b else placed("k_got0", [P, N], U32, EARLY)
            nc.vector.tensor_copy(k_got[b][:], k_pool[b][:].bitcast(U32).indirect(listed(b)))

        def part_keys(b):
            k_codes[b] = sb(f"k_codes{b}", [P, PASSES, 2 * N], U8)
            nc.vector.tensor_copy(
                out=k_codes[b][:].bitcast(U16),
                in_=k_got[b][:].bitcast(U16).rearrange("p (i o) -> p o i", o=PASSES),
            )

        def gather_values(b, h, tag=""):
            v_got = sb(f"v_got{b}{h}", [P, N], BF16, tag=tag)
            nc.scalar.activation(out=v_got[:], in_=v_pool[b, h][:].indirect(listed(b)), func=ACT.Copy)
            return v_got

        def gather_token_scales(b, tag=""):
            vs_got = sb(f"vs_got{b}", [P, N], F32, tag=tag)
            nc.scalar.activation(out=vs_got[:], in_=vs_pool[:].indirect(listed(b)), func=ACT.Copy)
            return vs_got

        def move_token_scales(b, vs_got):
            vs_cols[b] = placed(f"vs_cols{b}", [P, 8], F32, b * N)
            nc.sync.dma_start(out=vs_cols[b][:, 0:PACK], in_=vs_got[VS_ROW : VS_ROW + 1, :])

        nc.sync.dma_start(offsets[:], offs)
        nc.sync.dma_start(
            out=ks_pool[KS_ROW0:P, :].bitcast(I32), in_=k_scales.rearrange("o f t -> f o t").bitcast(I32)
        )
        load_keys(0)
        for quad in QUADS:
            nc.sync.dma_start(
                out=q_planes[32 * quad : 32 * quad + 4, :].bitcast(I32).rearrange("f (g q) -> f g q", g=B * PASSES),
                in_=q_scales[:, :, 4 * quad : 4 * quad + 4, :].rearrange("b o f q -> f (b o) q").bitcast(I32),
            )
        nc.sync.dma_start(out=vs_pool[VS_ROW : VS_ROW + 1, :], in_=vs[0:1, :])
        load_values(0, 0)
        nc.sync.dma_start(
            out=sink_rows[SINK_ROW : SINK_ROW + TILES, :], in_=sink.rearrange("b (h p) one -> (b h) (p one)", p=P)
        )
        load_keys(1)
        load_queries(0)

        move_key_scales(0, gather_key_scales(0))
        gather_keys(0)
        load_values(0, 1, tag="k_pool0")
        second_scales = gather_key_scales(1)
        load_queries(1, tag="ks_pool")
        move_key_scales(1, second_scales)
        part_keys(0)
        gather_keys(1)
        part_keys(1)
        og_rows = og.rearrange("b (h p) e -> p (b h) e", p=P)
        og_first = placed("og_first", [P, 1, DV], F32, EARLY)
        nc.sync.dma_start(out=og_first[:], in_=og_rows[:, 0:1, :])
        load_values(1, 0)
        vs_cols = {}
        move_token_scales(0, gather_token_scales(0))
        v_got = {(0, 0): gather_values(0, 0)}
        second_row = gather_token_scales(1, tag="v_pool00")
        load_values(1, 1, tag="k_pool1")
        move_token_scales(1, second_row)
        og_rest = sb("og_rest", [P, TILES - 1, DV], F32, tag="k_codes0")
        nc.sync.dma_start(out=og_rest[:], in_=og_rows[:, 1:TILES, :])
        og_sb = [og_first[:, 0, :]] + [og_rest[:, j, :] for j in range(TILES - 1)]

        def share_values(b, h, v_got):
            shares = [listed(b)[:, c * LIST_COLS // 2 : (c + 1) * LIST_COLS // 2] for c in range(2)]
            nc.scalar.activation(out=v_got[:, 0 : N // 2], in_=v_pool[b, h][:].indirect(shares[0]), func=ACT.Copy)
            return v_got, lambda: nc.vector.tensor_copy(v_got[:, N // 2 : N], v_pool[b, h][:].indirect(shares[1]))

        def turn_values(got, bank, woven, copy):
            turned = psum.tile([P, 2, P], F32, name="v_turned", tag=f"bank{bank}")
            words = got[:].bitcast(F32)
            for u in range(2):
                nc.tensor.transpose(turned[:, u, :], words[:, u : N // 2 : 2], ident[:])
            copy(
                out=woven.rearrange("p e t -> p (e t)").bitcast(F32).rearrange("p (e u) -> p e u", u=2),
                in_=turned[:].rearrange("p u e -> p e u"),
            )

        def scores(b, h, k_codes):
            acc = psum.tile([P, N], F32, name="score", tag=f"bank{b * HALVES + h}")
            for o in range(PASSES):
                first = (b * PASSES + o) * NQ + h * P
                nc.tensor.matmul_mx(
                    out=acc[:],
                    lhsT=q_codes[b][:, o, h * P : (h + 1) * P].bitcast(FP8X4),
                    lhsT_scale=q_planes[:, first : first + P],
                    rhs=k_codes[:, o, :].bitcast(FP4X4),
                    rhs_scale=k_planes[b][:, o * N : (o + 1) * N],
                    start=(o == 0),
                    stop=(o == PASSES - 1),
                )
            return acc

        def softmax(j, acc):
            neg_max = sb(f"neg_max{j}", [P, 1], F32)
            nc.vector.tensor_scalar(
                out=neg_logits[:, j, 0:N].rearrange("p (t s) -> p t s", t=PACK),
                in0=acc[:].rearrange("p (s t) -> p t s", t=PACK),
                scalar1=-1.0,
                scalar2=neg_logits[:, j, N : N + 1],
                op0=ALU.mult,
                op1=ALU.min,
                accum_out=neg_max[:],
            )
            probs = placed("probs1", [P, ROW], F32, N + 64) if j == 1 else sb(f"probs{j}", [P, ROW], F32)
            nc.scalar.activation(
                out=probs[:, 0 : N + 1],
                in_=neg_logits[:, j, 0 : N + 1],
                func=ACT.Exp,
                bias=neg_max[:],
                scale=-1.0,
                accum_out=totals[:, j : j + 1],
            )
            turned = psum.tile([P, PACK, P], F32, name="probs_turned", tag=f"bank{PROB_BANKS[j]}")
            for t in range(PACK):
                nc.tensor.transpose(turned[:, t, :], probs[:, t * P : (t + 1) * P], ident[:])
            return turned

        def quantize(name, woven, cols, tag=""):
            codes = sb(f"{name}_codes", [P, cols], U32, tag=tag)
            plane = sb(f"{name}_plane", [P, cols], U8)
            nc.vector.quantize_mx(
                out=codes[:].bitcast(FP8X4), scales=plane[:], in_=woven[:].rearrange("p c t -> p (c t)")
            )
            return codes, plane

        def weigh(j, turned):
            b, h = divmod(j, HALVES)
            nc.vector.tensor_tensor(
                out=w_woven[b][:, h * P : (h + 1) * P, :],
                in0=turned[:].rearrange("p t q -> p q t"),
                in1=vs_cols[b][:, 0:PACK].unsqueeze(1).to_broadcast([P, P, PACK]),
                op=ALU.mult,
            )

        def mix(b, w_mx, v_parts):
            accs = [psum.tile([P, DV], F32, name="mixed", tag=f"bank{MIX_BANKS[b * HALVES + h]}") for h in range(HALVES)]
            width = DV // len(v_parts)
            for c, v_mx in enumerate(v_parts):
                for h in range(HALVES):
                    rows = slice(h * P, (h + 1) * P)
                    nc.tensor.matmul_mx(
                        out=accs[h][:, c * width : (c + 1) * width],
                        lhsT=w_mx[0][:, rows].bitcast(FP8X4),
                        lhsT_scale=w_mx[1][:, rows],
                        rhs=v_mx[0][:].bitcast(FP8X4),
                        rhs_scale=v_mx[1][:],
                        start=True,
                        stop=True,
                    )
            return accs

        def finish(j, acc):
            result = sb(f"result{j}", [P, DV], F32)
            nc.vector.scalar_tensor_tensor(
                out=result[:],
                in0=acc[:],
                scalar=inverses[:, j : j + 1],
                in1=gate[:, j * DV : (j + 1) * DV],
                op0=ALU.mult,
                op1=ALU.mult,
            )
            b, h = divmod(j, HALVES)
            nc.sync.dma_start(out=out[b, h * P : (h + 1) * P, :], in_=result[:])

        def make_gate(tiles, tag):
            half_tanh = sb(f"half_tanh{tiles[0]}", [P, len(tiles), DV], F32, tag=tag)
            for c, j in enumerate(tiles):
                nc.scalar.activation(out=half_tanh[:, c, :], in_=og_sb[j], func=ACT.Tanh, scale=0.5)
                cols = slice(j * DV, (j + 1) * DV)
                if j < TILES - 1:
                    nc.gpsimd.tensor_scalar(
                        out=gate[:, cols], in0=half_tanh[:, c, :], scalar1=0.5, scalar2=0.5, op0=ALU.mult, op1=ALU.add
                    )
                else:
                    nc.scalar.activation(out=gate[:, cols], in_=half_tanh[:, c, :], func=ACT.Copy, scale=0.5, bias=0.5)

        first_woven = [sb(f"first_woven{h}", [P, P, PACK], BF16) for h in range(PLANES)]
        turn_values(v_got[0, 0], 7, first_woven[0][:], nc.scalar.copy)
        first_codes = placed("first_codes", [P, DV], U32, SECOND_GOT + 2 * N)
        first_plane = sb("first_plane", [P, DV], U8)

        def quantize_first(h):
            cols = slice(h * P, (h + 1) * P)
            nc.vector.quantize_mx(
                out=first_codes[:, cols].bitcast(FP8X4),
                scales=first_plane[:, cols],
                in_=first_woven[h][:].rearrange("p c t -> p (c t)"),
            )

        quantize_first(0)
        sink_turned = psum.tile([P, P], F32, name="sink_turned", tag="bank6")
        nc.tensor.transpose(sink_turned[:], sink_rows[:], ident[:])
        nc.scalar.activation(out=neg_logits[:, :, N], in_=sink_turned[:, SINK_ROW : SINK_ROW + TILES], func=ACT.Copy, scale=-1.0)
        v_got[0, 1], vector_share = share_values(0, 1, placed("v_got01", [P, N], BF16, SECOND_GOT))
        accs = [scores(b, h, k_codes[b]) for b in range(B) for h in range(HALVES)]
        soft = [softmax(0, accs[0])]
        vector_share()
        make_gate(range(1), tag="")
        soft.extend(softmax(j, accs[j]) for j in range(1, TILES))
        v_got[1, 0], vector_share = share_values(1, 0, sb("v_got10", [P, N], BF16, tag="neg_max1"))
        vector_share()
        v_got[1, 1] = gather_values(1, 1, tag="neg_max2")
        turn_values(v_got[0, 1], 1, first_woven[1][:], nc.scalar.copy)
        third_woven = sb("third_woven", [P, P, PACK], BF16)
        turn_values(v_got[1, 0], 2, third_woven[:], nc.scalar.copy)
        make_gate(range(1, 2), tag="k_pool1")
        last_woven = sb("last_woven", [P, P, PACK], BF16)
        turn_values(v_got[1, 1], 3, last_woven[:], nc.scalar.copy)
        make_gate(range(HALVES, TILES), tag="neg_max2")
        inverses = placed("inverses", [P, TILES], F32, EARLY + 4 * DV)
        nc.gpsimd.tensor_tensor(out=inverses[:], in0=totals[:], in1=minus_one[:], op=ALU.pow)
        w_woven = [sb(f"w_woven{b}", [P, NQ, PACK], BF16) for b in range(B)]
        for j in range(TILES):
            weigh(j, soft[j])
        w_mx = [quantize("w0", w_woven[0], NQ, tag=f"probs{TILES - 1}")]
        quantize_first(1)
        w_mx.append(quantize("w1", w_woven[1], NQ))
        second_woven = [third_woven, last_woven]
        v_mx = [
            [(first_codes, first_plane)],
            [quantize(f"v1{h}", second_woven[h], P) for h in range(PLANES)],
        ]
        mixed = [acc for b in range(B) for acc in mix(b, w_mx[b], v_mx[b])]
        for j in range(TILES):
            finish(j, mixed[j])
